import numpy as np
import ml_dtypes


def mxq(x, axis, fmt="e4m3"):
    dtype, down = {"e4m3": (ml_dtypes.float8_e4m3fn, 7), "e5m2": (ml_dtypes.float8_e5m2, 14)}[fmt]
    v = np.moveaxis(np.asarray(x, np.float32).astype(ml_dtypes.bfloat16).astype(np.float64), axis, -1)
    blocks = v.reshape(v.shape[:-1] + (-1, 32))
    amax = np.abs(blocks).max(-1, keepdims=True)
    byte = np.maximum(np.where(amax > 0, np.frexp(amax)[1] - 1 + 127, 0) - down, 1)
    scale = np.exp2(byte - 127.0)
    codes = (blocks / scale).astype(np.float32).astype(dtype).astype(np.float64)
    return np.moveaxis((codes * scale).reshape(v.shape), -1, axis)


WIDE = False


def mx_kscale(k):
    if not WIDE:
        return np.ones(k)
    levels = np.array([10, -10, 5, -5, 0])
    if k % 512:
        return np.exp2(np.random.permutation(np.resize(levels, k // 32))).repeat(32)
    a = np.empty((k // 512, 16))
    for p in range(k // 512):
        a[p, :8] = np.random.permutation(np.resize(levels, 8))
        for g in range(8):
            far = levels[np.abs(levels - a[p, g]) >= 10]
            a[p, g + 8] = far[np.random.randint(len(far))]
    return np.exp2(a.ravel()).repeat(32)


def f64(x):
    return np.asarray(x).astype(np.float64)


def striped(idx):
    return np.tile(idx.reshape(-1, 16).T, (8, 1)).astype(np.uint16)


def unstriped(offs):
    return offs[:16].T.reshape(-1).astype(np.int64)


E2M1 = np.array([0.0, 0.5, 1.0, 1.5, 2.0, 3.0, 4.0, 6.0, -0.0, -0.5, -1.0, -1.5, -2.0, -3.0, -4.0, -6.0])


def pack_weight(w, fmt):
    k, n = w.shape
    w = f64(np.asarray(w, np.float32).astype(ml_dtypes.bfloat16)).reshape(k // 32, 32, n)
    amax = np.abs(w).max(1)
    if fmt == "e4m3":
        byte = np.frexp(amax)[1] - 1 + 127 - 7
    else:
        mant, ex = np.frexp(amax / 6.0)
        byte = np.where(mant > 0.5, ex, ex - 1) + 127
    byte = np.clip(np.where(amax > 0, byte, 1), 1, 254)
    scaled = (w * np.exp2(127.0 - byte)[:, None, :]).reshape(k, n).astype(np.float32)
    by_word = np.ascontiguousarray(scaled.reshape(k // 512, 128, 4, n).transpose(0, 1, 3, 2))
    if fmt == "e4m3":
        words = by_word.astype(ml_dtypes.float8_e4m3fn).view(np.uint8)
    else:
        c = by_word.astype(ml_dtypes.float4_e2m1fn).view(np.uint8) & 0xF
        words = (c[..., 0::2] | (c[..., 1::2] << 4)).reshape(k // 512, 128, 2 * n)
    return np.ascontiguousarray(words), np.ascontiguousarray(byte.astype(np.uint8).reshape(k // 512, 16, n))


def unpack_weight(words, scales, fmt):
    g, _, n = scales.shape
    words = np.ascontiguousarray(words).reshape(g, 128, n, -1)
    if fmt == "e4m3":
        vals = words.view(ml_dtypes.float8_e4m3fn).astype(np.float64)
    else:
        nib = np.empty((g, 128, n, 4), np.uint8)
        nib[..., 0::2] = words & 0xF
        nib[..., 1::2] = words >> 4
        vals = E2M1[nib]
    vals = vals * np.repeat(np.exp2(scales.astype(np.float64) - 127.0), 8, axis=1)[..., None]
    return vals.transpose(0, 1, 3, 2).reshape(g * 512, n)


def gelu(v):
    return 0.5 * v * (1.0 + np.tanh(np.sqrt(2.0 / np.pi) * (v + 0.044715 * v**3)))


K, T, S, P, H, N = 1024, 2048, 1024, 512, 1536, 512

def setup_inputs():
    n = np.random.standard_normal
    s = mx_kscale(K)[:, None]
    u = mx_kscale(H)[:, None]
    tab_words, tab_scales = pack_weight(n((K, T)) * s, "e4m3")
    w1 = 2.0 * n((K, H)) / np.sqrt(K) / s
    gain = np.exp(0.3 * n(H)) * u[:, 0]
    w2_words, w2_scales = pack_weight(n((H, N)) / np.sqrt(H) / u, "e2m1")
    return {
        "tab_words": tab_words, "tab_scales": tab_scales,
        "offs": striped(np.random.permutation(T)[:S]),
        "w1": w1.astype(np.float32),
        "pos1": striped(np.random.permutation(S)[:P]),
        "pos2": striped(np.random.permutation(S)[:P]),
        "pos3": striped(np.random.permutation(S)[:P]),
        "gain": gain.astype(np.float32),
        "w2_words": w2_words, "w2_scales": w2_scales,
    }

def reference(tab_words, tab_scales, offs, w1, pos1, pos2, pos3, gain, w2_words, w2_scales):
    v = unpack_weight(tab_words, tab_scales, "e4m3")[:, unstriped(offs)]
    w2 = unpack_weight(w2_words, w2_scales, "e2m1")
    h = mxq(f64(w1), 0, "e4m3").T @ v
    x = np.stack([h[:, unstriped(pos1)], h[:, unstriped(pos2)], h[:, unstriped(pos3)]])
    a, b, c = 1.0 / (1.0 + np.exp(-x))
    med = np.maximum(np.minimum(a, b), np.minimum(np.maximum(a, b), c))
    z = f64(gain)[:, None] * med
    return w2.T @ mxq(z, 0, "e4m3")

@@ -1,0 +1,265 @@
+from contextlib import ExitStack
+
+import concourse.mybir as mybir
+
+K, T, S, PICKS, H, N = 1024, 2048, 1024, 512, 1536, 512
+FLOPS = 2 * K * H * S + 2 * H * N * PICKS
+
+F32 = mybir.dt.float32
+BF16 = mybir.dt.bfloat16
+I32 = mybir.dt.int32
+U32 = mybir.dt.uint32
+U16 = mybir.dt.uint16
+U8 = mybir.dt.uint8
+E4M3 = mybir.dt.float8_e4m3fn_x4
+E2M1 = mybir.dt.float4_e2m1fn_x4
+ALU = mybir.AluOpType
+SIGMOID = mybir.ActivationFunctionType.Sigmoid
+
+P = 128
+PACK = 4
+PASS = P * PACK
+BANK = 512
+K_PASSES = K // PASS
+GROUPS = H // PASS
+TILES = GROUPS * PACK
+SIDE = PICKS // 2
+
+
+def pieces(g, a):
+    return 2 if (g, a) == (0, K_PASSES - 1) else 1
+
+
+def tile_list_skating_panel_median_kernel(
+    tc, tab_words, tab_scales, offs, w1, pos1, pos2, pos3, gain, w2_words, w2_scales, out
+):
+    nc = tc.nc
+    with ExitStack() as ctx:
+        keep = ctx.enter_context(tc.tile_pool(name="keep", bufs=1))
+        ring = ctx.enter_context(tc.tile_pool(name="ring", bufs=2))
+        psum = ctx.enter_context(tc.psum_pool(name="psum", bufs=1))
+
+        idx = keep.tile([P, S // 16], U16, name="idx")
+        picks = [keep.tile([P, PICKS // 16], U16, name="pick%d" % i) for i in range(3)]
+        table = [keep.tile([P, T], I32, name="table%d" % a) for a in range(K_PASSES)]
+        table_sc = keep.tile([P, T], U8, name="table_sc")
+        raw = {}
+        gains = keep.tile([P, GROUPS, PACK], F32, name="gains")
+        w2_codes = keep.tile([P, GROUPS, 2 * N], U8, name="w2_codes", align_bytes=64)
+        w2_sc = keep.tile([P, GROUPS, N], U8, name="w2_sc", align_bytes=64)
+        warm = keep.tile([P, 8], F32, name="warm")
+
+        nc.gpsimd.memset(table_sc[:].bitcast(I32), 0)
+        nc.vector.memset(warm[:], 0.0)
+        nc.scalar.activation(warm[:, 0:1], warm[:, 1:2], SIGMOID)
+        nc.vector.memset(w2_sc[:].bitcast(I32), 0)
+
+        def load_w1(g, a):
+            width = PASS // pieces(g, a)
+            raw[g, a] = keep.tile([P, pieces(g, a), PACK, width], F32, name="raw%d" % a)
+            for u in range(pieces(g, a)):
+                c0 = g * PASS + u * width
+                rows = w1[a * PASS : (a + 1) * PASS, c0 : c0 + width]
+                nc.sync.dma_start(out=raw[g, a][:, u], in_=rows.rearrange("(p j) c -> p j c", j=PACK))
+
+        def load_table(a):
+            nc.sync.dma_start(
+                out=table[a][:], in_=tab_words[a].rearrange("p n t -> p (n t)").bitcast(I32)
+            )
+
+        nc.sync.dma_start(idx[:], offs)
+        for q in range(4):
+            nc.sync.dma_start(
+                out=table_sc[32 * q : 32 * q + 4 * K_PASSES, :].bitcast(I32),
+                in_=tab_scales[:, 4 * q : 4 * q + 4, :].bitcast(I32),
+            )
+        load_table(0)
+        load_w1(0, 0)
+        load_table(1)
+        load_w1(0, 1)
+        for tile_, src in zip(picks, (pos1, pos2, pos3)):
+            nc.sync.dma_start(tile_[:], src)
+        nc.sync.dma_start(out=gains[:], in_=gain.rearrange("(g p t) -> p g t", p=P, t=PACK))
+        nc.sync.dma_start(
+            out=w2_codes[:].bitcast(I32), in_=w2_words.rearrange("g p c -> p g c").bitcast(I32)
+        )
+        for q in range(4):
+            nc.sync.dma_start(
+                out=w2_sc[32 * q : 32 * q + 4, :, :].bitcast(I32),
+                in_=w2_scales[:, 4 * q : 4 * q + 4, :].rearrange("g r c -> r g c").bitcast(I32),
+            )
+
+        v_codes = [keep.tile([P, S], U32, name="v_codes%d" % a, align_bytes=64) for a in range(K_PASSES)]
+        v_sc = keep.tile([P, S], U8, name="v_sc", align_bytes=64)
+        nc.vector.tensor_copy(v_codes[0][:], table[0][:].bitcast(U32).indirect(idx[:]))
+        nc.vector.tensor_copy(v_sc[:], table_sc[:].indirect(idx[:]))
+        nc.vector.tensor_copy(v_codes[1][:], table[1][:].bitcast(U32).indirect(idx[:]))
+
+        w1_codes, w1_sc, rounded = {}, {}, {}
+
+        def round_w1(g, a, *copies):
+            rounded[g, a] = ring.tile([P, PACK, P, PACK], BF16, name="rounded", bufs=3, align_bytes=64)
+            width = P // len(copies)
+            for u, copy in enumerate(copies):
+                copy(
+                    rounded[g, a][:, :, u * width : (u + 1) * width, :].rearrange("p t m j -> p m j t"),
+                    raw[g, a][:, u].rearrange("p j (m t) -> p m j t", t=PACK),
+                )
+            if g + 1 < GROUPS:
+                load_w1(g + 1, a)
+
+        def quantise_w1(g, a, cuts=(0, PACK)):
+            w1_codes[g, a] = keep.tile([P, PASS], U32, name="w1_codes%d%d" % (g, a), align_bytes=64)
+            w1_sc[g, a] = keep.tile([P, PASS], U8, name="w1_sc%d%d" % (g, a), align_bytes=64)
+            for t0, t1 in zip(cuts, cuts[1:]):
+                nc.vector.quantize_mx(
+                    out=w1_codes[g, a][:, t0 * P : t1 * P].bitcast(E4M3),
+                    scales=w1_sc[g, a][:, t0 * P : t1 * P],
+                    in_=rounded[g, a][:, t0:t1].rearrange("p t m j -> p (t m j)"),
+                )
+
+        h = {}
+
+        def first_product(i):
+            g, t = divmod(i, PACK)
+            cols = slice(t * P, (t + 1) * P)
+            h[i] = ring.tile([P, S], F32, name="h", bufs=6)
+            acc = [psum.tile([P, BANK], F32, name="acc%d" % half, bufs=2) for half in range(2)]
+            parts = [slice(half * BANK, (half + 1) * BANK) for half in range(2)]
+            for a in range(K_PASSES):
+                for half, part in enumerate(parts):
+                    nc.tensor.matmul_mx(
+                        out=acc[half][:],
+                        lhsT=w1_codes[g, a][:, cols].bitcast(E4M3),
+                        lhsT_scale=w1_sc[g, a][:, cols],
+                        rhs=v_codes[a][:, part].bitcast(E4M3),
+                        rhs_scale=v_sc[4 * a :, part],
+                        start=(a == 0),
+                        stop=(a == K_PASSES - 1),
+                    )
+            copy = nc.vector.tensor_copy if i in (9, 10) else nc.scalar.copy
+            copy(h[i][:, parts[0]], acc[0][:])
+            nc.vector.tensor_copy(h[i][:, parts[1]], acc[1][:])
+
+        first, third, second, high = {}, {}, {}, {}
+
+        def look_up(i, cols):
+            g, t = divmod(i, PACK)
+            if g not in first:
+                first[g] = ring.tile([P, PACK, PICKS], F32, name="first", bufs=3)
+                third[g] = ring.tile([P, PACK, PICKS], F32, name="third", bufs=3)
+            if i not in second:
+                second[i] = ring.tile([P, PICKS], F32, name="second", bufs=4)
+            entries = slice(cols.start // 16, cols.stop // 16)
+            for dst, pick in zip((second[i][:, cols], first[g][:, t, cols], third[g][:, t, cols]), picks):
+                nc.scalar.activation(dst, h[i][:].indirect(pick[:, entries]), SIGMOID)
+
+        def weigh_second(i, cols):
+            g, t = divmod(i, PACK)
+            b = second[i][:, cols]
+            nc.vector.tensor_scalar(b, b, gains[:, g, t : t + 1], None, ALU.mult)
+
+        def sort_pair(i, cols):
+            g, t = divmod(i, PACK)
+            w = gains[:, g, t : t + 1]
+            if i not in high:
+                high[i] = ring.tile([P, PICKS], F32, name="high")
+            a, b = first[g][:, t, cols], second[i][:, cols]
+            nc.vector.scalar_tensor_tensor(high[i][:, cols], a, w, b, ALU.mult, ALU.max)
+            nc.vector.scalar_tensor_tensor(a, a, w, b, ALU.mult, ALU.min)
+
+        def clip_third(i, cols):
+            g, t = divmod(i, PACK)
+            c = third[g][:, t, cols]
+            nc.vector.scalar_tensor_tensor(c, c, gains[:, g, t : t + 1], high[i][:, cols], ALU.mult, ALU.min)
+
+        z, z_codes, z_sc, marks = {}, {}, {}, {}
+
+        def median(g, cols):
+            if g not in z:
+                z[g] = ring.tile([P, PICKS, PACK], BF16, name="z", align_bytes=64)
+            nc.vector.tensor_tensor(
+                z[g][:, cols, :].rearrange("p (c i) t -> p c t i", i=4),
+                first[g][:, :, cols].rearrange("p t (c i) -> p c t i", i=4),
+                third[g][:, :, cols].rearrange("p t (c i) -> p c t i", i=4),
+                ALU.max,
+            )
+
+        def quantise_z(g, cols):
+            if g not in z_codes:
+                z_codes[g] = keep.tile([P, PICKS], U32, name="z_codes%d" % g, align_bytes=64)
+                z_sc[g] = keep.tile([P, PICKS], U8, name="z_sc%d" % g, align_bytes=64)
+            nc.vector.quantize_mx(
+                out=z_codes[g][:, cols].bitcast(E4M3),
+                scales=z_sc[g][:, cols],
+                in_=z[g][:, cols, :].rearrange("p m t -> p (m t)"),
+            )
+
+        def second_product(g, half):
+            for n in range(N // P):
+                if g == 0:
+                    if half == 0:
+                        marks[n, half] = psum.tile([P, BANK], F32, name="marks%d" % n)
+                    else:
+                        marks[n, half] = psum.tile([P, BANK], F32, name="acc%d" % (n % 2), bufs=2)
+                for u in range(SIDE // P):
+                    cols = slice(half * SIDE + u * P, half * SIDE + (u + 1) * P)
+                    nc.tensor.matmul_mx(
+                        out=marks[n, half][:, u * P : (u + 1) * P],
+                        lhsT=w2_codes[:, g, 2 * P * n : 2 * P * (n + 1)].bitcast(E2M1),
+                        lhsT_scale=w2_sc[:, g, P * n : P * (n + 1)],
+                        rhs=z_codes[g][:, cols].bitcast(E4M3),
+                        rhs_scale=z_sc[g][:, cols],
+                        start=(g == 0 and u == 0),
+                        stop=(g == GROUPS - 1 and u == SIDE // P - 1),
+                    )
+
+        def store(half):
+            for n in range(N // P):
+                result = ring.tile([P, SIDE], F32, name="result", bufs=8)
+                copy = nc.scalar.copy if half == 0 or n % 2 == 0 else nc.vector.tensor_copy
+                copy(result[:], marks[n, half][:, :SIDE])
+                nc.sync.dma_start(
+                    out=out[n * P : (n + 1) * P, half * SIDE : (half + 1) * SIDE], in_=result[:]
+                )
+
+        whole = slice(0, PICKS)
+        sides = [slice(0, SIDE), slice(SIDE, PICKS)]
+        steps = [(i, whole) for i in range(TILES - 1)] + [(TILES - 1, side) for side in sides]
+
+        round_w1(0, 0, nc.scalar.copy)
+        round_w1(0, 1, nc.scalar.copy, nc.vector.tensor_copy)
+        quantise_w1(0, 0)
+        quantise_w1(0, 1, (0, 1, 2, PACK))
+        first_product(0)
+        first_product(1)
+        look_up(*steps[0])
+        weigh_second(*steps[0])
+        for step, (i, cols) in enumerate(steps):
+            g, t = divmod(i, PACK)
+            ahead = steps[step + 1] if step + 1 < len(steps) else None
+            if g + 1 < GROUPS and t < K_PASSES:
+                round_w1(g + 1, t, nc.vector.tensor_copy)
+            if i + 2 < TILES:
+                first_product(i + 2)
+            if g + 1 < GROUPS and t < K_PASSES:
+                quantise_w1(g + 1, t)
+            if ahead:
+                look_up(*ahead)
+            sort_pair(i, cols)
+            if t == 0 and g > 0:
+                quantise_z(g - 1, whole)
+                second_product(g - 1, 0)
+            if ahead:
+                weigh_second(*ahead)
+            if i == TILES - 2:
+                for earlier in range(GROUPS - 1):
+                    second_product(earlier, 1)
+            clip_third(i, cols)
+            if t == PACK - 1:
+                median(g, cols)
+            if i == TILES - 1:
+                half = cols.start // SIDE
+                quantise_z(g, cols)
+                second_product(g, half)
+                store(half)

@@ -97,33 +97,37 @@ def tile_list_skating_panel_median_kernel(
 
         w1_codes, w1_sc, rounded = {}, {}, {}
 
-        def round_w1(g, a, *copies):
-            rounded[g, a] = ring.tile([P, PACK, P, PACK], BF16, name="rounded", bufs=3, align_bytes=64)
-            width = P // len(copies)
-            for u, copy in enumerate(copies):
-                copy(
-                    rounded[g, a][:, :, u * width : (u + 1) * width, :].rearrange("p t m j -> p m j t"),
-                    raw[g, a][:, u].rearrange("p j (m t) -> p m j t", t=PACK),
-                )
-            if g + 1 < GROUPS:
+        def round_w1(g, a, pair, copy, by_piece=False):
+            if pair == 0:
+                rounded[g, a] = ring.tile([P, PACK, P, PACK], BF16, name="rounded", bufs=3, align_bytes=64)
+            n = pieces(g, a)
+            ts = slice(2 * pair, 2 * pair + 2)
+            dst = rounded[g, a][:, ts].rearrange("p t (u m) j -> p u m j t", u=n)
+            src = raw[g, a][:].rearrange("p u j (m t) -> p u m j t", t=PACK)[:, :, :, :, ts]
+            if by_piece or n == 1:
+                for u in range(n):
+                    copy(dst[:, u], src[:, u])
+            else:
+                copy(dst, src)
+            if pair == 1 and g + 1 < GROUPS:
                 load_w1(g + 1, a)
 
-        def quantise_w1(g, a, cuts=(0, PACK)):
-            w1_codes[g, a] = keep.tile([P, PASS], U32, name="w1_codes%d%d" % (g, a), align_bytes=64)
-            w1_sc[g, a] = keep.tile([P, PASS], U8, name="w1_sc%d%d" % (g, a), align_bytes=64)
-            for t0, t1 in zip(cuts, cuts[1:]):
-                nc.vector.quantize_mx(
-                    out=w1_codes[g, a][:, t0 * P : t1 * P].bitcast(E4M3),
-                    scales=w1_sc[g, a][:, t0 * P : t1 * P],
-                    in_=rounded[g, a][:, t0:t1].rearrange("p t m j -> p (t m j)"),
-                )
+        def quantise_w1(g, a, t0, t1):
+            if t0 == 0:
+                w1_codes[g, a] = keep.tile([P, PASS], U32, name="w1_codes%d%d" % (g, a), align_bytes=64)
+                w1_sc[g, a] = keep.tile([P, PASS], U8, name="w1_sc%d%d" % (g, a), align_bytes=64)
+            nc.vector.quantize_mx(
+                out=w1_codes[g, a][:, t0 * P : t1 * P].bitcast(E4M3),
+                scales=w1_sc[g, a][:, t0 * P : t1 * P],
+                in_=rounded[g, a][:, t0:t1].rearrange("p t m j -> p (t m j)"),
+            )
 
         h = {}
 
         def first_product(i):
             g, t = divmod(i, PACK)
             cols = slice(t * P, (t + 1) * P)
-            h[i] = ring.tile([P, S], F32, name="h", bufs=6)
+            h[i] = ring.tile([P, S], F32, name="h", bufs=TILES)
             acc = [psum.tile([P, BANK], F32, name="acc%d" % half, bufs=2) for half in range(2)]
             parts = [slice(half * BANK, (half + 1) * BANK) for half in range(2)]
             for a in range(K_PASSES):
@@ -137,73 +141,76 @@ def tile_list_skating_panel_median_kernel(
                         start=(a == 0),
                         stop=(a == K_PASSES - 1),
                     )
-            copy = nc.vector.tensor_copy if i in (9, 10) else nc.scalar.copy
-            copy(h[i][:, parts[0]], acc[0][:])
-            nc.vector.tensor_copy(h[i][:, parts[1]], acc[1][:])
+            copies = [nc.scalar.copy, nc.vector.tensor_copy]
+            if 0 < i < PACK:
+                copies[0] = nc.vector.tensor_copy
+            if i >= TILES - 2:
+                copies[1] = nc.scalar.copy
+            for half, part in enumerate(parts):
+                copies[half](h[i][:, part], acc[half][:])
 
-        first, third, second, high = {}, {}, {}, {}
+        first, third, second, high, z = {}, {}, {}, {}, {}
 
         def look_up(i, cols):
             g, t = divmod(i, PACK)
-            if g not in first:
-                first[g] = ring.tile([P, PACK, PICKS], F32, name="first", bufs=3)
-                third[g] = ring.tile([P, PACK, PICKS], F32, name="third", bufs=3)
-            if i not in second:
-                second[i] = ring.tile([P, PICKS], F32, name="second", bufs=4)
+            width = cols.stop - cols.start
+            if t == 0:
+                first[g, cols.start] = keep.tile([P, PACK, width], F32, name="first%d_%d" % (g, cols.start))
+                third[g, cols.start] = keep.tile([P, PACK, width], F32, name="third%d_%d" % (g, cols.start))
+            second[i, cols.start] = keep.tile([P, width], F32, name="second%d_%d" % (i, cols.start))
             entries = slice(cols.start // 16, cols.stop // 16)
-            for dst, pick in zip((second[i][:, cols], first[g][:, t, cols], third[g][:, t, cols]), picks):
+            dsts = (second[i, cols.start][:], first[g, cols.start][:, t], third[g, cols.start][:, t])
+            for dst, pick in zip(dsts, picks):
                 nc.scalar.activation(dst, h[i][:].indirect(pick[:, entries]), SIGMOID)
 
         def weigh_second(i, cols):
             g, t = divmod(i, PACK)
-            b = second[i][:, cols]
+            b = second[i, cols.start][:]
             nc.vector.tensor_scalar(b, b, gains[:, g, t : t + 1], None, ALU.mult)
 
         def sort_pair(i, cols):
             g, t = divmod(i, PACK)
             w = gains[:, g, t : t + 1]
-            if i not in high:
-                high[i] = ring.tile([P, PICKS], F32, name="high")
-            a, b = first[g][:, t, cols], second[i][:, cols]
-            nc.vector.scalar_tensor_tensor(high[i][:, cols], a, w, b, ALU.mult, ALU.max)
+            high[i] = ring.tile([P, cols.stop - cols.start], F32, name="high")
+            a, b = first[g, cols.start][:, t], second[i, cols.start][:]
+            nc.vector.scalar_tensor_tensor(high[i][:], a, w, b, ALU.mult, ALU.max)
             nc.vector.scalar_tensor_tensor(a, a, w, b, ALU.mult, ALU.min)
 
         def clip_third(i, cols):
             g, t = divmod(i, PACK)
-            c = third[g][:, t, cols]
-            nc.vector.scalar_tensor_tensor(c, c, gains[:, g, t : t + 1], high[i][:, cols], ALU.mult, ALU.min)
+            c = third[g, cols.start][:, t]
+            nc.vector.scalar_tensor_tensor(c, c, gains[:, g, t : t + 1], high[i][:], ALU.mult, ALU.min)
 
-        z, z_codes, z_sc, marks = {}, {}, {}, {}
+        z_codes = [keep.tile([P, PICKS], U32, name="z_codes%d" % g, align_bytes=64) for g in range(GROUPS)]
+        z_sc = [keep.tile([P, PICKS], U8, name="z_sc%d" % g, align_bytes=64) for g in range(GROUPS)]
+        marks = {}
 
-        def median(g, cols):
-            if g not in z:
-                z[g] = ring.tile([P, PICKS, PACK], BF16, name="z", align_bytes=64)
+        def median(g, cols, part):
+            inside = slice(part.start - cols.start, part.stop - cols.start)
+            z[g, part.start] = ring.tile([P, part.stop - part.start, PACK], BF16, name="z", align_bytes=64)
             nc.vector.tensor_tensor(
-                z[g][:, cols, :].rearrange("p (c i) t -> p c t i", i=4),
-                first[g][:, :, cols].rearrange("p t (c i) -> p c t i", i=4),
-                third[g][:, :, cols].rearrange("p t (c i) -> p c t i", i=4),
+                z[g, part.start][:].rearrange("p (c i) t -> p c t i", i=2),
+                first[g, cols.start][:, :, inside].rearrange("p t (c i) -> p c t i", i=2),
+                third[g, cols.start][:, :, inside].rearrange("p t (c i) -> p c t i", i=2),
                 ALU.max,
             )
 
-        def quantise_z(g, cols):
-            if g not in z_codes:
-                z_codes[g] = keep.tile([P, PICKS], U32, name="z_codes%d" % g, align_bytes=64)
-                z_sc[g] = keep.tile([P, PICKS], U8, name="z_sc%d" % g, align_bytes=64)
+        def quantise_z(g, part):
             nc.vector.quantize_mx(
-                out=z_codes[g][:, cols].bitcast(E4M3),
-                scales=z_sc[g][:, cols],
-                in_=z[g][:, cols, :].rearrange("p m t -> p (m t)"),
+                out=z_codes[g][:, part].bitcast(E4M3),
+                scales=z_sc[g][:, part],
+                in_=z[g, part.start][:].rearrange("p m t -> p (m t)"),
             )
 
         def second_product(g, half):
-            for n in range(N // P):
-                if g == 0:
-                    if half == 0:
-                        marks[n, half] = psum.tile([P, BANK], F32, name="marks%d" % n)
-                    else:
-                        marks[n, half] = psum.tile([P, BANK], F32, name="acc%d" % (n % 2), bufs=2)
-                for u in range(SIDE // P):
-                    cols = slice(half * SIDE + u * P, half * SIDE + (u + 1) * P)
+            for u in range(SIDE // P):
+                cols = slice(half * SIDE + u * P, half * SIDE + (u + 1) * P)
+                for n in range(N // P):
+                    if g == 0 and u == 0:
+                        if half == 0:
+                            marks[n, half] = psum.tile([P, BANK], F32, name="marks%d" % n)
+                        else:
+                            marks[n, half] = psum.tile([P, BANK], F32, name="acc%d" % (n % 2), bufs=2)
                     nc.tensor.matmul_mx(
                         out=marks[n, half][:, u * P : (u + 1) * P],
                         lhsT=w2_codes[:, g, 2 * P * n : 2 * P * (n + 1)].bitcast(E2M1),
@@ -225,41 +232,57 @@ def tile_list_skating_panel_median_kernel(
 
         whole = slice(0, PICKS)
         sides = [slice(0, SIDE), slice(SIDE, PICKS)]
-        steps = [(i, whole) for i in range(TILES - 1)] + [(TILES - 1, side) for side in sides]
+        last = range(TILES - PACK, TILES)
+        steps = [(i, whole) for i in range(TILES - PACK)] + [(i, side) for side in sides for i in last]
 
-        round_w1(0, 0, nc.scalar.copy)
-        round_w1(0, 1, nc.scalar.copy, nc.vector.tensor_copy)
-        quantise_w1(0, 0)
-        quantise_w1(0, 1, (0, 1, 2, PACK))
+        for pair in range(2):
+            round_w1(0, 0, pair, nc.scalar.copy)
+        round_w1(0, 1, 0, nc.scalar.copy, by_piece=True)
+        round_w1(0, 1, 1, nc.scalar.copy)
+        quantise_w1(0, 0, 0, 2)
+        quantise_w1(0, 1, 0, 1)
         first_product(0)
+        quantise_w1(0, 1, 1, 2)
         first_product(1)
+        quantise_w1(0, 0, 2, 4)
+        quantise_w1(0, 1, 2, 4)
         look_up(*steps[0])
         weigh_second(*steps[0])
+        made = 2
+        finished = None
         for step, (i, cols) in enumerate(steps):
             g, t = divmod(i, PACK)
             ahead = steps[step + 1] if step + 1 < len(steps) else None
             if g + 1 < GROUPS and t < K_PASSES:
-                round_w1(g + 1, t, nc.vector.tensor_copy)
-            if i + 2 < TILES:
-                first_product(i + 2)
+                for pair in range(2):
+                    round_w1(g + 1, t, pair, nc.vector.tensor_copy)
+            for tile_no in range(made, min(TILES, step + 3 + (step >= TILES - PACK - 1))):
+                first_product(tile_no)
+                made = tile_no + 1
             if g + 1 < GROUPS and t < K_PASSES:
-                quantise_w1(g + 1, t)
+                quantise_w1(g + 1, t, 0, PACK)
             if ahead:
                 look_up(*ahead)
             sort_pair(i, cols)
-            if t == 0 and g > 0:
-                quantise_z(g - 1, whole)
-                second_product(g - 1, 0)
+            if finished:
+                quantise_z(*finished)
+                second_product(finished[0], 0)
+                if finished[0] == GROUPS - 1:
+                    store(0)
+                finished = None
             if ahead:
                 weigh_second(*ahead)
-            if i == TILES - 2:
+            if step == TILES - 2:
                 for earlier in range(GROUPS - 1):
                     second_product(earlier, 1)
             clip_third(i, cols)
-            if t == PACK - 1:
-                median(g, cols)
-            if i == TILES - 1:
-                half = cols.start // SIDE
-                quantise_z(g, cols)
-                second_product(g, half)
-                store(half)
+            if t == PACK - 1 and ahead:
+                median(g, cols, cols)
+                finished = (g, cols)
+        ends = [slice(c, c + P) for c in range(SIDE, PICKS, P)]
+        for part in ends:
+            median(GROUPS - 1, sides[1], part)
+        for part in ends:
+            quantise_z(GROUPS - 1, part)
+        second_product(GROUPS - 1, 1)
+        store(1)

@@ -141,57 +141,58 @@ def tile_list_skating_panel_median_kernel(
                         start=(a == 0),
                         stop=(a == K_PASSES - 1),
                     )
-            copies = [nc.scalar.copy, nc.vector.tensor_copy]
-            if 0 < i < PACK:
-                copies[0] = nc.vector.tensor_copy
-            if i >= TILES - 2:
-                copies[1] = nc.scalar.copy
+            copies = [nc.scalar.copy if i == 0 else nc.vector.tensor_copy, nc.vector.tensor_copy]
             for half, part in enumerate(parts):
                 copies[half](h[i][:, part], acc[half][:])
 
         first, third, second, high, z = {}, {}, {}, {}, {}
 
+        def plane(tiles, i, cols):
+            g, t = divmod(i, PACK)
+            return tiles[g][:, t * PICKS + cols.start : t * PICKS + cols.stop]
+
         def look_up(i, cols):
             g, t = divmod(i, PACK)
-            width = cols.stop - cols.start
             if t == 0:
-                first[g, cols.start] = keep.tile([P, PACK, width], F32, name="first%d_%d" % (g, cols.start))
-                third[g, cols.start] = keep.tile([P, PACK, width], F32, name="third%d_%d" % (g, cols.start))
-            second[i, cols.start] = keep.tile([P, width], F32, name="second%d_%d" % (i, cols.start))
+                first[g] = keep.tile([P, PACK * PICKS], F32, name="first%d" % g)
+                third[g] = keep.tile([P, PACK * PICKS], F32, name="third%d" % g)
+            second[i, cols.start] = keep.tile(
+                [P, cols.stop - cols.start], F32, name="second%d_%d" % (i, cols.start)
+            )
             entries = slice(cols.start // 16, cols.stop // 16)
-            dsts = (second[i, cols.start][:], first[g, cols.start][:, t], third[g, cols.start][:, t])
+            dsts = (second[i, cols.start][:], plane(first, i, cols), plane(third, i, cols))
             for dst, pick in zip(dsts, picks):
                 nc.scalar.activation(dst, h[i][:].indirect(pick[:, entries]), SIGMOID)
 
-        def weigh_second(i, cols):
+        def gain_of(i):
             g, t = divmod(i, PACK)
+            return gains[:, g, t : t + 1]
+
+        def weigh_second(i, cols):
             b = second[i, cols.start][:]
-            nc.vector.tensor_scalar(b, b, gains[:, g, t : t + 1], None, ALU.mult)
+            nc.vector.tensor_scalar(b, b, gain_of(i), None, ALU.mult)
 
         def sort_pair(i, cols):
-            g, t = divmod(i, PACK)
-            w = gains[:, g, t : t + 1]
             high[i] = ring.tile([P, cols.stop - cols.start], F32, name="high")
-            a, b = first[g, cols.start][:, t], second[i, cols.start][:]
-            nc.vector.scalar_tensor_tensor(high[i][:], a, w, b, ALU.mult, ALU.max)
-            nc.vector.scalar_tensor_tensor(a, a, w, b, ALU.mult, ALU.min)
+            a, b = plane(first, i, cols), second[i, cols.start][:]
+            nc.vector.scalar_tensor_tensor(high[i][:], a, gain_of(i), b, ALU.mult, ALU.max)
+            nc.vector.scalar_tensor_tensor(a, a, gain_of(i), b, ALU.mult, ALU.min)
 
         def clip_third(i, cols):
-            g, t = divmod(i, PACK)
-            c = third[g, cols.start][:, t]
-            nc.vector.scalar_tensor_tensor(c, c, gains[:, g, t : t + 1], high[i][:], ALU.mult, ALU.min)
+            c = plane(third, i, cols)
+            nc.vector.scalar_tensor_tensor(c, c, gain_of(i), high[i][:], ALU.mult, ALU.min)
 
         z_codes = [keep.tile([P, PICKS], U32, name="z_codes%d" % g, align_bytes=64) for g in range(GROUPS)]
         z_sc = [keep.tile([P, PICKS], U8, name="z_sc%d" % g, align_bytes=64) for g in range(GROUPS)]
         marks = {}
 
-        def median(g, cols, part):
-            inside = slice(part.start - cols.start, part.stop - cols.start)
+        def median(g, part):
             z[g, part.start] = ring.tile([P, part.stop - part.start, PACK], BF16, name="z", align_bytes=64)
+            pairs = slice(part.start // 2, part.stop // 2)
             nc.vector.tensor_tensor(
                 z[g, part.start][:].rearrange("p (c i) t -> p c t i", i=2),
-                first[g, cols.start][:, :, inside].rearrange("p t (c i) -> p c t i", i=2),
-                third[g, cols.start][:, :, inside].rearrange("p t (c i) -> p c t i", i=2),
+                first[g][:].rearrange("p (t c i) -> p c t i", t=PACK, i=2)[:, pairs],
+                third[g][:].rearrange("p (t c i) -> p c t i", t=PACK, i=2)[:, pairs],
                 ALU.max,
             )
 
@@ -232,8 +233,7 @@ def tile_list_skating_panel_median_kernel(
 
         whole = slice(0, PICKS)
         sides = [slice(0, SIDE), slice(SIDE, PICKS)]
-        last = range(TILES - PACK, TILES)
-        steps = [(i, whole) for i in range(TILES - PACK)] + [(i, side) for side in sides for i in last]
+        steps = [(i, whole) for i in range(TILES - 1)] + [(TILES - 1, side) for side in sides]
 
         for pair in range(2):
             round_w1(0, 0, pair, nc.scalar.copy)
@@ -248,7 +248,6 @@ def tile_list_skating_panel_median_kernel(
         quantise_w1(0, 1, 2, 4)
         look_up(*steps[0])
         weigh_second(*steps[0])
-        made = 2
         finished = None
         for step, (i, cols) in enumerate(steps):
             g, t = divmod(i, PACK)
@@ -256,9 +255,8 @@ def tile_list_skating_panel_median_kernel(
             if g + 1 < GROUPS and t < K_PASSES:
                 for pair in range(2):
                     round_w1(g + 1, t, pair, nc.vector.tensor_copy)
-            for tile_no in range(made, min(TILES, step + 3 + (step >= TILES - PACK - 1))):
-                first_product(tile_no)
-                made = tile_no + 1
+            if step + 2 < TILES:
+                first_product(step + 2)
             if g + 1 < GROUPS and t < K_PASSES:
                 quantise_w1(g + 1, t, 0, PACK)
             if ahead:
@@ -277,11 +275,11 @@ def tile_list_skating_panel_median_kernel(
                     second_product(earlier, 1)
             clip_third(i, cols)
             if t == PACK - 1 and ahead:
-                median(g, cols, cols)
+                median(g, cols)
                 finished = (g, cols)
         ends = [slice(c, c + P) for c in range(SIDE, PICKS, P)]
         for part in ends:
-            median(GROUPS - 1, sides[1], part)
+            median(GROUPS - 1, part)
         for part in ends:
             quantise_z(GROUPS - 1, part)
         second_product(GROUPS - 1, 1)

@@ -141,7 +141,7 @@ def tile_list_skating_panel_median_kernel(
                         start=(a == 0),
                         stop=(a == K_PASSES - 1),
                     )
-            copies = [nc.scalar.copy if i == 0 else nc.vector.tensor_copy, nc.vector.tensor_copy]
+            copies = [nc.scalar.copy if i == 0 or (i > PACK and i % 2 == 1) else nc.vector.tensor_copy, nc.vector.tensor_copy]
             for half, part in enumerate(parts):
                 copies[half](h[i][:, part], acc[half][:])
 

@@ -24,6 +24,8 @@ K_PASSES = K // PASS
 GROUPS = H // PASS
 TILES = GROUPS * PACK
 SIDE = PICKS // 2
+SCALAR_TILE = PACK + 2
+AHEAD = 3
 
 
 def pieces(g, a):
@@ -56,7 +58,7 @@ def tile_list_skating_panel_median_kernel(
 
         def load_w1(g, a):
             width = PASS // pieces(g, a)
-            raw[g, a] = keep.tile([P, pieces(g, a), PACK, width], F32, name="raw%d" % a)
+            raw[g, a] = ring.tile([P, pieces(g, a), PACK, width], F32, name="raw%d" % a)
             for u in range(pieces(g, a)):
                 c0 = g * PASS + u * width
                 rows = w1[a * PASS : (a + 1) * PASS, c0 : c0 + width]
@@ -80,6 +82,8 @@ def tile_list_skating_panel_median_kernel(
         for tile_, src in zip(picks, (pos1, pos2, pos3)):
             nc.sync.dma_start(tile_[:], src)
         nc.sync.dma_start(out=gains[:], in_=gain.rearrange("(g p t) -> p g t", p=P, t=PACK))
+        for a in range(K_PASSES):
+            load_w1(1, a)
         nc.sync.dma_start(
             out=w2_codes[:].bitcast(I32), in_=w2_words.rearrange("g p c -> p g c").bitcast(I32)
         )
@@ -99,7 +103,7 @@ def tile_list_skating_panel_median_kernel(
 
         def round_w1(g, a, pair, copy, by_piece=False):
             if pair == 0:
-                rounded[g, a] = ring.tile([P, PACK, P, PACK], BF16, name="rounded", bufs=3, align_bytes=64)
+                rounded[g, a] = ring.tile([P, PACK, P, PACK], BF16, name="rounded", bufs=4, align_bytes=64)
             n = pieces(g, a)
             ts = slice(2 * pair, 2 * pair + 2)
             dst = rounded[g, a][:, ts].rearrange("p t (u m) j -> p u m j t", u=n)
@@ -109,8 +113,8 @@ def tile_list_skating_panel_median_kernel(
                     copy(dst[:, u], src[:, u])
             else:
                 copy(dst, src)
-            if pair == 1 and g + 1 < GROUPS:
-                load_w1(g + 1, a)
+            if pair == 1 and g + 2 < GROUPS:
+                load_w1(g + 2, a)
 
         def quantise_w1(g, a, t0, t1):
             if t0 == 0:
@@ -124,10 +128,12 @@ def tile_list_skating_panel_median_kernel(
 
         h = {}
 
+        banks = {}
+
         def first_product(i):
             g, t = divmod(i, PACK)
             cols = slice(t * P, (t + 1) * P)
-            h[i] = ring.tile([P, S], F32, name="h", bufs=TILES)
+            h[i] = ring.tile([P, S], F32, name="h", bufs=AHEAD + 1)
             acc = [psum.tile([P, BANK], F32, name="acc%d" % half, bufs=2) for half in range(2)]
             parts = [slice(half * BANK, (half + 1) * BANK) for half in range(2)]
             for a in range(K_PASSES):
@@ -141,11 +147,14 @@ def tile_list_skating_panel_median_kernel(
                         start=(a == 0),
                         stop=(a == K_PASSES - 1),
                     )
-            copies = [nc.scalar.copy if i == 0 or (i > PACK and i % 2 == 1) else nc.vector.tensor_copy, nc.vector.tensor_copy]
-            for half, part in enumerate(parts):
-                copies[half](h[i][:, part], acc[half][:])
+            banks[i] = acc
 
-        first, third, second, high, z = {}, {}, {}, {}, {}
+        def empty_bank(i, half):
+            on_scalar = (half == 0 and i == 0) or i == SCALAR_TILE
+            copy = nc.scalar.copy if on_scalar else nc.vector.tensor_copy
+            copy(h[i][:, half * BANK : (half + 1) * BANK], banks[i][half][:])
+
+        first, third, second, high, low, z = {}, {}, {}, {}, {}, {}
 
         def plane(tiles, i, cols):
             g, t = divmod(i, PACK)
@@ -168,15 +177,29 @@ def tile_list_skating_panel_median_kernel(
             g, t = divmod(i, PACK)
             return gains[:, g, t : t + 1]
 
-        def weigh_second(i, cols):
-            b = second[i, cols.start][:]
-            nc.vector.tensor_scalar(b, b, gain_of(i), None, ALU.mult)
+        weighed = {}
 
-        def sort_pair(i, cols):
+        def weigh_second(i, cols, beside_copies=False):
+            b = second[i, cols.start][:]
+            if beside_copies:
+                scaled = keep.tile([P, PICKS], F32, name="scaled")
+                nc.gpsimd.tensor_scalar(scaled[:], b, gain_of(i), 0.0, ALU.mult, ALU.add)
+                weighed[i, cols.start] = scaled[:]
+            else:
+                nc.vector.tensor_scalar(b, b, gain_of(i), None, ALU.mult)
+                weighed[i, cols.start] = b
+
+        def upper(i, cols):
             high[i] = ring.tile([P, cols.stop - cols.start], F32, name="high")
-            a, b = plane(first, i, cols), second[i, cols.start][:]
+            a, b = plane(first, i, cols), weighed[i, cols.start]
             nc.vector.scalar_tensor_tensor(high[i][:], a, gain_of(i), b, ALU.mult, ALU.max)
-            nc.vector.scalar_tensor_tensor(a, a, gain_of(i), b, ALU.mult, ALU.min)
+
+        def lower(i, cols):
+            g, t = divmod(i, PACK)
+            if t == 0:
+                low[g] = ring.tile([P, PACK * PICKS], F32, name="low")
+            a, b = plane(first, i, cols), weighed[i, cols.start]
+            nc.vector.scalar_tensor_tensor(plane(low, i, cols), a, gain_of(i), b, ALU.mult, ALU.min)
 
         def clip_third(i, cols):
             c = plane(third, i, cols)
@@ -191,7 +214,7 @@ def tile_list_skating_panel_median_kernel(
             pairs = slice(part.start // 2, part.stop // 2)
             nc.vector.tensor_tensor(
                 z[g, part.start][:].rearrange("p (c i) t -> p c t i", i=2),
-                first[g][:].rearrange("p (t c i) -> p c t i", t=PACK, i=2)[:, pairs],
+                low[g][:].rearrange("p (t c i) -> p c t i", t=PACK, i=2)[:, pairs],
                 third[g][:].rearrange("p (t c i) -> p c t i", t=PACK, i=2)[:, pairs],
                 ALU.max,
             )
@@ -203,37 +226,50 @@ def tile_list_skating_panel_median_kernel(
                 in_=z[g, part.start][:].rearrange("p m t -> p (m t)"),
             )
 
-        def second_product(g, half):
-            for u in range(SIDE // P):
-                cols = slice(half * SIDE + u * P, half * SIDE + (u + 1) * P)
-                for n in range(N // P):
-                    if g == 0 and u == 0:
-                        if half == 0:
-                            marks[n, half] = psum.tile([P, BANK], F32, name="marks%d" % n)
-                        else:
-                            marks[n, half] = psum.tile([P, BANK], F32, name="acc%d" % (n % 2), bufs=2)
-                    nc.tensor.matmul_mx(
-                        out=marks[n, half][:, u * P : (u + 1) * P],
-                        lhsT=w2_codes[:, g, 2 * P * n : 2 * P * (n + 1)].bitcast(E2M1),
-                        lhsT_scale=w2_sc[:, g, P * n : P * (n + 1)],
-                        rhs=z_codes[g][:, cols].bitcast(E4M3),
-                        rhs_scale=z_sc[g][:, cols],
-                        start=(g == 0 and u == 0),
-                        stop=(g == GROUPS - 1 and u == SIDE // P - 1),
-                    )
+        whole = slice(0, PICKS)
+        sides = [slice(0, SIDE), slice(SIDE, SIDE + P), slice(SIDE + P, PICKS)]
+        steps = [(i, whole) for i in range(TILES - 1)] + [(TILES - 1, side) for side in sides]
 
-        def store(half):
-            for n in range(N // P):
-                result = ring.tile([P, SIDE], F32, name="result", bufs=8)
-                copy = nc.scalar.copy if half == 0 or n % 2 == 0 else nc.vector.tensor_copy
-                copy(result[:], marks[n, half][:, :SIDE])
-                nc.sync.dma_start(
-                    out=out[n * P : (n + 1) * P, half * SIDE : (half + 1) * SIDE], in_=result[:]
+        def blocks_of(side):
+            return [(n, c) for c in range(side.start, side.stop, P) for n in range(N // P)]
+
+        def place(side, n, c):
+            if side.start == 0:
+                return n, c // P
+            return n // 2, n % 2
+
+        def second_product(g, side):
+            for n, c in blocks_of(side):
+                bank, slot = place(side, n, c)
+                if g == 0 and slot == 0:
+                    if side.start == 0:
+                        marks[side.start, bank] = psum.tile([P, BANK], F32, name="marks%d" % bank)
+                    else:
+                        marks[side.start, bank] = psum.tile([P, BANK], F32, name="acc%d" % bank, bufs=2)
+                nc.tensor.matmul_mx(
+                    out=marks[side.start, bank][:, slot * P : (slot + 1) * P],
+                    lhsT=w2_codes[:, g, 2 * P * n : 2 * P * (n + 1)].bitcast(E2M1),
+                    lhsT_scale=w2_sc[:, g, P * n : P * (n + 1)],
+                    rhs=z_codes[g][:, c : c + P].bitcast(E4M3),
+                    rhs_scale=z_sc[g][:, c : c + P],
+                    start=(g == 0 and slot == 0),
+                    stop=(g == GROUPS - 1 and slot == 1),
                 )
 
-        whole = slice(0, PICKS)
-        sides = [slice(0, SIDE), slice(SIDE, PICKS)]
-        steps = [(i, whole) for i in range(TILES - 1)] + [(TILES - 1, side) for side in sides]
+        def store(side):
+            for bank in range(N // P if side.start == 0 else 2):
+                result = ring.tile([P, SIDE], F32, name="result", bufs=8)
+                last = side.stop == PICKS and bank == 1
+                copy = nc.vector.tensor_copy if last else nc.scalar.copy
+                copy(result[:], marks[side.start, bank][:, :SIDE])
+                if side.start == 0:
+                    nc.sync.dma_start(out=out[bank * P : (bank + 1) * P, side], in_=result[:])
+                else:
+                    rows = out[2 * bank * P : 2 * (bank + 1) * P, side]
+                    nc.sync.dma_start(
+                        out=rows.rearrange("(n p) m -> p n m", p=P),
+                        in_=result[:].rearrange("p (n m) -> p n m", n=2),
+                    )
 
         for pair in range(2):
             round_w1(0, 0, pair, nc.scalar.copy)
@@ -242,45 +278,66 @@ def tile_list_skating_panel_median_kernel(
         quantise_w1(0, 0, 0, 2)
         quantise_w1(0, 1, 0, 1)
         first_product(0)
+        for half in range(2):
+            empty_bank(0, half)
         quantise_w1(0, 1, 1, 2)
         first_product(1)
+        for half in range(2):
+            empty_bank(1, half)
         quantise_w1(0, 0, 2, 4)
         quantise_w1(0, 1, 2, 4)
+        first_product(2)
+        for half in range(2):
+            empty_bank(2, half)
         look_up(*steps[0])
         weigh_second(*steps[0])
         finished = None
         for step, (i, cols) in enumerate(steps):
             g, t = divmod(i, PACK)
             ahead = steps[step + 1] if step + 1 < len(steps) else None
-            if g + 1 < GROUPS and t < K_PASSES:
-                for pair in range(2):
-                    round_w1(g + 1, t, pair, nc.vector.tensor_copy)
-            if step + 2 < TILES:
-                first_product(step + 2)
-            if g + 1 < GROUPS and t < K_PASSES:
-                quantise_w1(g + 1, t, 0, PACK)
+            coming = step + AHEAD
+            beside_copies = coming < TILES and coming != SCALAR_TILE
+            casts = g + 1 < GROUPS and t % 2 == 0
+            if coming < TILES:
+                first_product(coming)
+            if step + 2 == SCALAR_TILE:
+                for half in range(2):
+                    empty_bank(step + 2, half)
             if ahead:
                 look_up(*ahead)
-            sort_pair(i, cols)
+            upper(i, cols)
+            if finished:
+                median(*finished)
+            if g > 0 and t == 1:
+                median(g - 1, whole)
+            lower(i, cols)
+            if beside_copies:
+                weigh_second(*ahead, beside_copies=True)
+                for half in range(2):
+                    empty_bank(coming, half)
             if finished:
                 quantise_z(*finished)
-                second_product(finished[0], 0)
-                if finished[0] == GROUPS - 1:
-                    store(0)
-                finished = None
-            if ahead:
+                second_product(*finished)
+                store(finished[1])
+            if g > 0 and t == 1:
+                quantise_z(g - 1, whole)
+                second_product(g - 1, sides[0])
+            if ahead and not beside_copies:
                 weigh_second(*ahead)
+            if casts:
+                for a in range(K_PASSES):
+                    round_w1(g + 1, a, t // 2, nc.vector.tensor_copy)
             if step == TILES - 2:
-                for earlier in range(GROUPS - 1):
-                    second_product(earlier, 1)
+                for side in sides[1:]:
+                    for earlier in range(GROUPS - 1):
+                        second_product(earlier, side)
             clip_third(i, cols)
-            if t == PACK - 1 and ahead:
-                median(g, cols)
+            if casts:
+                for a in range(K_PASSES):
+                    quantise_w1(g + 1, a, t, t + 2)
+            if i == TILES - 1:
                 finished = (g, cols)
-        ends = [slice(c, c + P) for c in range(SIDE, PICKS, P)]
-        for part in ends:
-            median(GROUPS - 1, part)
-        for part in ends:
-            quantise_z(GROUPS - 1, part)
-        second_product(GROUPS - 1, 1)
-        store(1)
+        median(*finished)
+        quantise_z(*finished)
+        second_product(*finished)
+        store(finished[1])

@@ -24,7 +24,7 @@ K_PASSES = K // PASS
 GROUPS = H // PASS
 TILES = GROUPS * PACK
 SIDE = PICKS // 2
-SCALAR_TILE = PACK + 2
+SCALAR_TILES = (2 * PACK, 2 * PACK + 2)
 AHEAD = 3
 
 
@@ -150,7 +150,7 @@ def tile_list_skating_panel_median_kernel(
             banks[i] = acc
 
         def empty_bank(i, half):
-            on_scalar = (half == 0 and i == 0) or i == SCALAR_TILE
+            on_scalar = (half == 0 and i == 0) or i in SCALAR_TILES
             copy = nc.scalar.copy if on_scalar else nc.vector.tensor_copy
             copy(h[i][:, half * BANK : (half + 1) * BANK], banks[i][half][:])
 
@@ -228,7 +228,8 @@ def tile_list_skating_panel_median_kernel(
 
         whole = slice(0, PICKS)
         sides = [slice(0, SIDE), slice(SIDE, SIDE + P), slice(SIDE + P, PICKS)]
-        steps = [(i, whole) for i in range(TILES - 1)] + [(TILES - 1, side) for side in sides]
+        steps = [(i, whole) for i in range(TILES - 2)]
+        steps = steps + [(i, cols) for cols in (sides[0], slice(SIDE, PICKS)) for i in (TILES - 2, TILES - 1)]
 
         def blocks_of(side):
             return [(n, c) for c in range(side.start, side.stop, P) for n in range(N // P)]
@@ -287,20 +288,22 @@ def tile_list_skating_panel_median_kernel(
         quantise_w1(0, 0, 2, 4)
         quantise_w1(0, 1, 2, 4)
         first_product(2)
+        look_up(*steps[0])
+        weigh_second(*steps[0], beside_copies=True)
         for half in range(2):
             empty_bank(2, half)
-        look_up(*steps[0])
-        weigh_second(*steps[0])
         finished = None
         for step, (i, cols) in enumerate(steps):
             g, t = divmod(i, PACK)
             ahead = steps[step + 1] if step + 1 < len(steps) else None
             coming = step + AHEAD
-            beside_copies = coming < TILES and coming != SCALAR_TILE
-            casts = g + 1 < GROUPS and t % 2 == 0
+            beside_copies = coming < TILES and coming not in SCALAR_TILES
+            later, pair = 1 + step // 2, step % 2
+            casts = later < GROUPS
+            closes = g > 0 and t == 0
             if coming < TILES:
                 first_product(coming)
-            if step + 2 == SCALAR_TILE:
+            if step + 2 in SCALAR_TILES:
                 for half in range(2):
                     empty_bank(step + 2, half)
             if ahead:
@@ -308,8 +311,6 @@ def tile_list_skating_panel_median_kernel(
             upper(i, cols)
             if finished:
                 median(*finished)
-            if g > 0 and t == 1:
-                median(g - 1, whole)
             lower(i, cols)
             if beside_copies:
                 weigh_second(*ahead, beside_copies=True)
@@ -319,14 +320,13 @@ def tile_list_skating_panel_median_kernel(
                 quantise_z(*finished)
                 second_product(*finished)
                 store(finished[1])
-            if g > 0 and t == 1:
-                quantise_z(g - 1, whole)
-                second_product(g - 1, sides[0])
+            if closes:
+                median(g - 1, whole)
             if ahead and not beside_copies:
                 weigh_second(*ahead)
             if casts:
                 for a in range(K_PASSES):
-                    round_w1(g + 1, a, t // 2, nc.vector.tensor_copy)
+                    round_w1(later, a, pair, nc.vector.tensor_copy)
             if step == TILES - 2:
                 for side in sides[1:]:
                     for earlier in range(GROUPS - 1):
@@ -334,10 +334,14 @@ def tile_list_skating_panel_median_kernel(
             clip_third(i, cols)
             if casts:
                 for a in range(K_PASSES):
-                    quantise_w1(g + 1, a, t, t + 2)
-            if i == TILES - 1:
-                finished = (g, cols)
-        median(*finished)
-        quantise_z(*finished)
-        second_product(*finished)
-        store(finished[1])
+                    quantise_w1(later, a, 2 * pair, 2 * pair + 2)
+            if closes:
+                quantise_z(g - 1, whole)
+                second_product(g - 1, sides[0])
+            finished = (g, cols) if i == TILES - 1 else None
+        for side in sides[1:]:
+            median(GROUPS - 1, side)
+        for side in sides[1:]:
+            quantise_z(GROUPS - 1, side)
+            second_product(GROUPS - 1, side)
+            store(side)

@@ -314,6 +314,7 @@ def tile_list_skating_panel_median_kernel(
             lower(i, cols)
             if beside_copies:
                 weigh_second(*ahead, beside_copies=True)
+                clip_third(i, cols)
                 for half in range(2):
                     empty_bank(coming, half)
             if finished:
@@ -325,13 +326,14 @@ def tile_list_skating_panel_median_kernel(
             if ahead and not beside_copies:
                 weigh_second(*ahead)
             if casts:
-                for a in range(K_PASSES):
-                    round_w1(later, a, pair, nc.vector.tensor_copy)
+                round_w1(later, 0, pair, nc.vector.tensor_copy)
+                round_w1(later, 1, pair, nc.vector.tensor_copy)
             if step == TILES - 2:
                 for side in sides[1:]:
                     for earlier in range(GROUPS - 1):
                         second_product(earlier, side)
-            clip_third(i, cols)
+            if not beside_copies:
+                clip_third(i, cols)
             if casts:
                 for a in range(K_PASSES):
                     quantise_w1(later, a, 2 * pair, 2 * pair + 2)

@@ -24,7 +24,7 @@ K_PASSES = K // PASS
 GROUPS = H // PASS
 TILES = GROUPS * PACK
 SIDE = PICKS // 2
-SCALAR_TILES = (2 * PACK, 2 * PACK + 2)
+SCALAR_TILES = (2 * PACK, 2 * PACK + 2, 2 * PACK + 3)
 AHEAD = 3
 
 
@@ -154,24 +154,39 @@ def tile_list_skating_panel_median_kernel(
             copy = nc.scalar.copy if on_scalar else nc.vector.tensor_copy
             copy(h[i][:, half * BANK : (half + 1) * BANK], banks[i][half][:])
 
-        first, third, second, high, low, z = {}, {}, {}, {}, {}, {}
+        first, third, second, high, low, clipped, z = {}, {}, {}, {}, {}, {}, {}
 
         def plane(tiles, i, cols):
             g, t = divmod(i, PACK)
             return tiles[g][:, t * PICKS + cols.start : t * PICKS + cols.stop]
 
+        def block(g):
+            return P if g == GROUPS - 1 else PICKS
+
+        def blocked(ap, g):
+            return ap.rearrange("p (b m) -> p b m", m=block(g))
+
+        def sorted_plane(tiles, i, cols):
+            g, t = divmod(i, PACK)
+            view = tiles[g][:].rearrange("p (b t m) -> p b t m", t=PACK, m=block(g))
+            return view[:, cols.start // block(g) : cols.stop // block(g), t]
+
+        def pick(dst, i, cols, judge):
+            entries = picks[judge][:, cols.start // 16 : cols.stop // 16]
+            nc.scalar.activation(dst, h[i][:].indirect(entries), SIGMOID)
+
         def look_up(i, cols):
             g, t = divmod(i, PACK)
             if t == 0:
-                first[g] = keep.tile([P, PACK * PICKS], F32, name="first%d" % g)
-                third[g] = keep.tile([P, PACK * PICKS], F32, name="third%d" % g)
+                first[g] = ring.tile([P, PACK * PICKS], F32, name="first")
+                third[g] = ring.tile([P, PACK * PICKS], F32, name="third")
             second[i, cols.start] = keep.tile(
                 [P, cols.stop - cols.start], F32, name="second%d_%d" % (i, cols.start)
             )
-            entries = slice(cols.start // 16, cols.stop // 16)
-            dsts = (second[i, cols.start][:], plane(first, i, cols), plane(third, i, cols))
-            for dst, pick in zip(dsts, picks):
-                nc.scalar.activation(dst, h[i][:].indirect(pick[:, entries]), SIGMOID)
+            pick(second[i, cols.start][:], i, cols, 0)
+            pick(plane(first, i, cols), i, cols, 1)
+            if cols.start == 0:
+                pick(plane(third, i, cols), i, cols, 2)
 
         def gain_of(i):
             g, t = divmod(i, PACK)
@@ -198,12 +213,16 @@ def tile_list_skating_panel_median_kernel(
             g, t = divmod(i, PACK)
             if t == 0:
                 low[g] = ring.tile([P, PACK * PICKS], F32, name="low")
-            a, b = plane(first, i, cols), weighed[i, cols.start]
-            nc.vector.scalar_tensor_tensor(plane(low, i, cols), a, gain_of(i), b, ALU.mult, ALU.min)
+                clipped[g] = ring.tile([P, PACK * PICKS], F32, name="clipped")
+            a, b = blocked(plane(first, i, cols), g), blocked(weighed[i, cols.start], g)
+            nc.vector.scalar_tensor_tensor(sorted_plane(low, i, cols), a, gain_of(i), b, ALU.mult, ALU.min)
 
         def clip_third(i, cols):
-            c = plane(third, i, cols)
-            nc.vector.scalar_tensor_tensor(c, c, gain_of(i), high[i][:], ALU.mult, ALU.min)
+            g = i // PACK
+            c = blocked(plane(third, i, cols), g)
+            origin = cols.start // SIDE * SIDE
+            bound = blocked(high[i][:, cols.start - origin : cols.stop - origin], g)
+            nc.vector.scalar_tensor_tensor(sorted_plane(clipped, i, cols), c, gain_of(i), bound, ALU.mult, ALU.min)
 
         z_codes = [keep.tile([P, PICKS], U32, name="z_codes%d" % g, align_bytes=64) for g in range(GROUPS)]
         z_sc = [keep.tile([P, PICKS], U8, name="z_sc%d" % g, align_bytes=64) for g in range(GROUPS)]
@@ -211,13 +230,15 @@ def tile_list_skating_panel_median_kernel(
 
         def median(g, part):
             z[g, part.start] = ring.tile([P, part.stop - part.start, PACK], BF16, name="z", align_bytes=64)
-            pairs = slice(part.start // 2, part.stop // 2)
-            nc.vector.tensor_tensor(
-                z[g, part.start][:].rearrange("p (c i) t -> p c t i", i=2),
-                low[g][:].rearrange("p (t c i) -> p c t i", t=PACK, i=2)[:, pairs],
-                third[g][:].rearrange("p (t c i) -> p c t i", t=PACK, i=2)[:, pairs],
-                ALU.max,
-            )
+            for c0 in range(part.start, part.stop, block(g)):
+                span = slice(PACK * c0, PACK * (c0 + block(g)))
+                dst = z[g, part.start][:, c0 - part.start : c0 - part.start + block(g)]
+                nc.vector.tensor_tensor(
+                    dst.rearrange("p (c i) t -> p c t i", i=2),
+                    low[g][:, span].rearrange("p (t c i) -> p c t i", t=PACK, i=2),
+                    clipped[g][:, span].rearrange("p (t c i) -> p c t i", t=PACK, i=2),
+                    ALU.max,
+                )
 
         def quantise_z(g, part):
             nc.vector.quantize_mx(
@@ -292,7 +313,7 @@ def tile_list_skating_panel_median_kernel(
         weigh_second(*steps[0], beside_copies=True)
         for half in range(2):
             empty_bank(2, half)
-        finished = None
+        finished = closed = None
         for step, (i, cols) in enumerate(steps):
             g, t = divmod(i, PACK)
             ahead = steps[step + 1] if step + 1 < len(steps) else None
@@ -309,6 +330,9 @@ def tile_list_skating_panel_median_kernel(
             if ahead:
                 look_up(*ahead)
             upper(i, cols)
+            if closed is not None:
+                quantise_z(closed, whole)
+                second_product(closed, sides[0])
             if finished:
                 median(*finished)
             lower(i, cols)
@@ -332,18 +356,26 @@ def tile_list_skating_panel_median_kernel(
                 for side in sides[1:]:
                     for earlier in range(GROUPS - 1):
                         second_product(earlier, side)
-            if not beside_copies:
+            if not beside_copies and cols.start == 0:
                 clip_third(i, cols)
             if casts:
                 for a in range(K_PASSES):
                     quantise_w1(later, a, 2 * pair, 2 * pair + 2)
-            if closes:
-                quantise_z(g - 1, whole)
-                second_product(g - 1, sides[0])
+            closed = g - 1 if closes else None
             finished = (g, cols) if i == TILES - 1 else None
+        last = GROUPS - 1
         for side in sides[1:]:
-            median(GROUPS - 1, side)
-        for side in sides[1:]:
-            quantise_z(GROUPS - 1, side)
-            second_product(GROUPS - 1, side)
-            store(side)
+            for i in (TILES - 2, TILES - 1):
+                pick(plane(third, i, side), i, side, 2)
+        clip_third(TILES - 2, sides[1])
+        clip_third(TILES - 1, sides[1])
+        clip_third(TILES - 2, sides[2])
+        median(last, sides[1])
+        clip_third(TILES - 1, sides[2])
+        quantise_z(last, sides[1])
+        second_product(last, sides[1])
+        store(sides[1])
+        median(last, sides[2])
+        quantise_z(last, sides[2])
+        second_product(last, sides[2])
+        store(sides[2])

@@ -24,7 +24,7 @@ K_PASSES = K // PASS
 GROUPS = H // PASS
 TILES = GROUPS * PACK
 SIDE = PICKS // 2
-SCALAR_TILES = (2 * PACK, 2 * PACK + 2, 2 * PACK + 3)
+SCALAR_TILES = (2 * PACK, 2 * PACK + 2)
 AHEAD = 3
 
 
@@ -116,6 +116,11 @@ def tile_list_skating_panel_median_kernel(
             if pair == 1 and g + 2 < GROUPS:
                 load_w1(g + 2, a)
 
+        def round_whole(g, a):
+            rounded[g, a] = ring.tile([P, PACK, P, PACK], BF16, name="rounded", bufs=4, align_bytes=64)
+            dst = rounded[g, a][:].rearrange("p t m j -> p m j t")
+            nc.vector.tensor_copy(dst, raw[g, a][:, 0].rearrange("p j (m t) -> p m j t", t=PACK))
+
         def quantise_w1(g, a, t0, t1):
             if t0 == 0:
                 w1_codes[g, a] = keep.tile([P, PASS], U32, name="w1_codes%d%d" % (g, a), align_bytes=64)
@@ -185,7 +190,7 @@ def tile_list_skating_panel_median_kernel(
             )
             pick(second[i, cols.start][:], i, cols, 0)
             pick(plane(first, i, cols), i, cols, 1)
-            if cols.start == 0:
+            if cols.start == 0 or i < TILES - 2:
                 pick(plane(third, i, cols), i, cols, 2)
 
         def gain_of(i):
@@ -197,7 +202,7 @@ def tile_list_skating_panel_median_kernel(
         def weigh_second(i, cols, beside_copies=False):
             b = second[i, cols.start][:]
             if beside_copies:
-                scaled = keep.tile([P, PICKS], F32, name="scaled")
+                scaled = keep.tile([P, cols.stop - cols.start], F32, name="scaled")
                 nc.gpsimd.tensor_scalar(scaled[:], b, gain_of(i), 0.0, ALU.mult, ALU.add)
                 weighed[i, cols.start] = scaled[:]
             else:
@@ -234,9 +239,9 @@ def tile_list_skating_panel_median_kernel(
                 span = slice(PACK * c0, PACK * (c0 + block(g)))
                 dst = z[g, part.start][:, c0 - part.start : c0 - part.start + block(g)]
                 nc.vector.tensor_tensor(
-                    dst.rearrange("p (c i) t -> p c t i", i=2),
-                    low[g][:, span].rearrange("p (t c i) -> p c t i", t=PACK, i=2),
-                    clipped[g][:, span].rearrange("p (t c i) -> p c t i", t=PACK, i=2),
+                    dst.rearrange("p (c i) t -> p c t i", i=4),
+                    low[g][:, span].rearrange("p (t c i) -> p c t i", t=PACK, i=4),
+                    clipped[g][:, span].rearrange("p (t c i) -> p c t i", t=PACK, i=4),
                     ALU.max,
                 )
 
@@ -311,16 +316,18 @@ def tile_list_skating_panel_median_kernel(
         first_product(2)
         look_up(*steps[0])
         weigh_second(*steps[0], beside_copies=True)
+        round_whole(1, 0)
         for half in range(2):
             empty_bank(2, half)
+        quantise_w1(1, 0, 0, PACK)
+        round_whole(1, 1)
+        waiting = (1, 1)
         finished = closed = None
         for step, (i, cols) in enumerate(steps):
             g, t = divmod(i, PACK)
             ahead = steps[step + 1] if step + 1 < len(steps) else None
             coming = step + AHEAD
             beside_copies = coming < TILES and coming not in SCALAR_TILES
-            later, pair = 1 + step // 2, step % 2
-            casts = later < GROUPS
             closes = g > 0 and t == 0
             if coming < TILES:
                 first_product(coming)
@@ -329,38 +336,39 @@ def tile_list_skating_panel_median_kernel(
                     empty_bank(step + 2, half)
             if ahead:
                 look_up(*ahead)
+            if finished:
+                median(*finished)
             upper(i, cols)
+            if waiting:
+                quantise_w1(*waiting, 0, PACK)
             if closed is not None:
                 quantise_z(closed, whole)
                 second_product(closed, sides[0])
             if finished:
-                median(*finished)
+                quantise_z(*finished)
+                second_product(*finished)
+                store(finished[1])
             lower(i, cols)
             if beside_copies:
                 weigh_second(*ahead, beside_copies=True)
                 clip_third(i, cols)
                 for half in range(2):
                     empty_bank(coming, half)
-            if finished:
-                quantise_z(*finished)
-                second_product(*finished)
-                store(finished[1])
+            if ahead and i == TILES - 1:
+                clip_third(i, cols)
             if closes:
                 median(g - 1, whole)
             if ahead and not beside_copies:
                 weigh_second(*ahead)
-            if casts:
-                round_w1(later, 0, pair, nc.vector.tensor_copy)
-                round_w1(later, 1, pair, nc.vector.tensor_copy)
+            waiting = (GROUPS - 1, step - 2) if step in (2, 3) else None
+            if waiting:
+                round_whole(*waiting)
             if step == TILES - 2:
                 for side in sides[1:]:
                     for earlier in range(GROUPS - 1):
                         second_product(earlier, side)
-            if not beside_copies and cols.start == 0:
+            if not beside_copies and (i < TILES - 2 or (i < TILES - 1 and cols.start == 0)):
                 clip_third(i, cols)
-            if casts:
-                for a in range(K_PASSES):
-                    quantise_w1(later, a, 2 * pair, 2 * pair + 2)
             closed = g - 1 if closes else None
             finished = (g, cols) if i == TILES - 1 else None
         last = GROUPS - 1

@@ -24,7 +24,7 @@ K_PASSES = K // PASS
 GROUPS = H // PASS
 TILES = GROUPS * PACK
 SIDE = PICKS // 2
-SCALAR_TILES = (2 * PACK, 2 * PACK + 2)
+SCALAR_TILES = range(2 * PACK - 1, TILES - 1)
 AHEAD = 3
 
 
@@ -155,7 +155,7 @@ def tile_list_skating_panel_median_kernel(
             banks[i] = acc
 
         def empty_bank(i, half):
-            on_scalar = (half == 0 and i == 0) or i in SCALAR_TILES
+            on_scalar = half == 0 and (i == 0 or i in SCALAR_TILES)
             copy = nc.scalar.copy if on_scalar else nc.vector.tensor_copy
             copy(h[i][:, half * BANK : (half + 1) * BANK], banks[i][half][:])
 
@@ -327,13 +327,12 @@ def tile_list_skating_panel_median_kernel(
             g, t = divmod(i, PACK)
             ahead = steps[step + 1] if step + 1 < len(steps) else None
             coming = step + AHEAD
-            beside_copies = coming < TILES and coming not in SCALAR_TILES
+            beside_copies = coming < TILES
             closes = g > 0 and t == 0
             if coming < TILES:
                 first_product(coming)
             if step + 2 in SCALAR_TILES:
-                for half in range(2):
-                    empty_bank(step + 2, half)
+                empty_bank(step + 2, 0)
             if ahead:
                 look_up(*ahead)
             if finished:
@@ -352,7 +351,7 @@ def tile_list_skating_panel_median_kernel(
             if beside_copies:
                 weigh_second(*ahead, beside_copies=True)
                 clip_third(i, cols)
-                for half in range(2):
+                for half in range(1 if coming in SCALAR_TILES else 0, 2):
                     empty_bank(coming, half)
             if ahead and i == TILES - 1:
                 clip_third(i, cols)

@@ -24,7 +24,7 @@ K_PASSES = K // PASS
 GROUPS = H // PASS
 TILES = GROUPS * PACK
 SIDE = PICKS // 2
-SCALAR_TILES = range(2 * PACK - 1, TILES - 1)
+SCALAR_TILES = (5, 6, 7, 11)
 AHEAD = 3
 
 

@@ -23,13 +23,10 @@ BANK = 512
 K_PASSES = K // PASS
 GROUPS = H // PASS
 TILES = GROUPS * PACK
+WHOLE_TILES = TILES - 2
 SIDE = PICKS // 2
-SCALAR_TILES = (5, 6, 7, 11)
+SCALAR_TILES = (6, 7, 9, 10, 11)
 AHEAD = 3
-
-
-def pieces(g, a):
-    return 2 if (g, a) == (0, K_PASSES - 1) else 1
 
 
 def tile_list_skating_panel_median_kernel(
@@ -45,7 +42,6 @@ def tile_list_skating_panel_median_kernel(
         picks = [keep.tile([P, PICKS // 16], U16, name="pick%d" % i) for i in range(3)]
         table = [keep.tile([P, T], I32, name="table%d" % a) for a in range(K_PASSES)]
         table_sc = keep.tile([P, T], U8, name="table_sc")
-        raw = {}
         gains = keep.tile([P, GROUPS, PACK], F32, name="gains")
         w2_codes = keep.tile([P, GROUPS, 2 * N], U8, name="w2_codes", align_bytes=64)
         w2_sc = keep.tile([P, GROUPS, N], U8, name="w2_sc", align_bytes=64)
@@ -56,13 +52,15 @@ def tile_list_skating_panel_median_kernel(
         nc.scalar.activation(warm[:, 0:1], warm[:, 1:2], SIGMOID)
         nc.vector.memset(w2_sc[:].bitcast(I32), 0)
 
-        def load_w1(g, a):
-            width = PASS // pieces(g, a)
-            raw[g, a] = ring.tile([P, pieces(g, a), PACK, width], F32, name="raw%d" % a)
-            for u in range(pieces(g, a)):
-                c0 = g * PASS + u * width
-                rows = w1[a * PASS : (a + 1) * PASS, c0 : c0 + width]
-                nc.sync.dma_start(out=raw[g, a][:, u], in_=rows.rearrange("(p j) c -> p j c", j=PACK))
+        raw = {}
+
+        def load_w1(g, a, u=0, n=1):
+            width = PASS // n
+            if u == 0:
+                raw[g, a] = keep.tile([P, n, PACK, width], F32, name="raw%d%d" % (g, a))
+            c0 = g * PASS + u * width
+            rows = w1[a * PASS : (a + 1) * PASS, c0 : c0 + width]
+            nc.sync.dma_start(out=raw[g, a][:, u], in_=rows.rearrange("(p j) c -> p j c", j=PACK))
 
         def load_table(a):
             nc.sync.dma_start(
@@ -70,20 +68,24 @@ def tile_list_skating_panel_median_kernel(
             )
 
         nc.sync.dma_start(idx[:], offs)
+        load_w1(0, 0, 0, 2)
+        nc.sync.dma_start(picks[0][:], pos1)
         for q in range(4):
             nc.sync.dma_start(
                 out=table_sc[32 * q : 32 * q + 4 * K_PASSES, :].bitcast(I32),
                 in_=tab_scales[:, 4 * q : 4 * q + 4, :].bitcast(I32),
             )
         load_table(0)
-        load_w1(0, 0)
+        load_w1(0, 0, 1, 2)
         load_table(1)
-        load_w1(0, 1)
-        for tile_, src in zip(picks, (pos1, pos2, pos3)):
-            nc.sync.dma_start(tile_[:], src)
+        load_w1(0, 1, 0, 2)
+        load_w1(0, 1, 1, 2)
+        nc.sync.dma_start(picks[1][:], pos2)
+        nc.sync.dma_start(picks[2][:], pos3)
         nc.sync.dma_start(out=gains[:], in_=gain.rearrange("(g p t) -> p g t", p=P, t=PACK))
-        for a in range(K_PASSES):
-            load_w1(1, a)
+        for g in range(1, GROUPS):
+            for a in range(K_PASSES):
+                load_w1(g, a)
         nc.sync.dma_start(
             out=w2_codes[:].bitcast(I32), in_=w2_words.rearrange("g p c -> p g c").bitcast(I32)
         )
@@ -95,33 +97,26 @@ def tile_list_skating_panel_median_kernel(
 
         v_codes = [keep.tile([P, S], U32, name="v_codes%d" % a, align_bytes=64) for a in range(K_PASSES)]
         v_sc = keep.tile([P, S], U8, name="v_sc", align_bytes=64)
-        nc.vector.tensor_copy(v_codes[0][:], table[0][:].bitcast(U32).indirect(idx[:]))
-        nc.vector.tensor_copy(v_sc[:], table_sc[:].indirect(idx[:]))
-        nc.vector.tensor_copy(v_codes[1][:], table[1][:].bitcast(U32).indirect(idx[:]))
 
         w1_codes, w1_sc, rounded = {}, {}, {}
 
-        def round_w1(g, a, pair, copy, by_piece=False):
-            if pair == 0:
-                rounded[g, a] = ring.tile([P, PACK, P, PACK], BF16, name="rounded", bufs=4, align_bytes=64)
-            n = pieces(g, a)
+        def round_lead(a, pair, u=None):
+            if (0, a) not in rounded:
+                rounded[0, a] = ring.tile([P, PACK, P, PACK], BF16, name="rounded", bufs=4, align_bytes=64)
             ts = slice(2 * pair, 2 * pair + 2)
-            dst = rounded[g, a][:, ts].rearrange("p t (u m) j -> p u m j t", u=n)
-            src = raw[g, a][:].rearrange("p u j (m t) -> p u m j t", t=PACK)[:, :, :, :, ts]
-            if by_piece or n == 1:
-                for u in range(n):
-                    copy(dst[:, u], src[:, u])
+            dst = rounded[0, a][:, ts].rearrange("p t (u m) j -> p u m j t", u=2)
+            src = raw[0, a][:].rearrange("p u j (m t) -> p u m j t", t=PACK)[:, :, :, :, ts]
+            if u is None:
+                nc.scalar.copy(dst, src)
             else:
-                copy(dst, src)
-            if pair == 1 and g + 2 < GROUPS:
-                load_w1(g + 2, a)
+                nc.scalar.copy(dst[:, u], src[:, u])
 
         def round_whole(g, a):
             rounded[g, a] = ring.tile([P, PACK, P, PACK], BF16, name="rounded", bufs=4, align_bytes=64)
             dst = rounded[g, a][:].rearrange("p t m j -> p m j t")
             nc.vector.tensor_copy(dst, raw[g, a][:, 0].rearrange("p j (m t) -> p m j t", t=PACK))
 
-        def quantise_w1(g, a, t0, t1):
+        def quantise_w1(g, a, t0=0, t1=PACK):
             if t0 == 0:
                 w1_codes[g, a] = keep.tile([P, PASS], U32, name="w1_codes%d%d" % (g, a), align_bytes=64)
                 w1_sc[g, a] = keep.tile([P, PASS], U8, name="w1_sc%d%d" % (g, a), align_bytes=64)
@@ -131,20 +126,25 @@ def tile_list_skating_panel_median_kernel(
                 in_=rounded[g, a][:, t0:t1].rearrange("p t m j -> p (t m j)"),
             )
 
-        h = {}
-
-        banks = {}
+        h, banks = {}, {}
 
         def first_product(i):
             g, t = divmod(i, PACK)
             cols = slice(t * P, (t + 1) * P)
             h[i] = ring.tile([P, S], F32, name="h", bufs=AHEAD + 1)
-            acc = [psum.tile([P, BANK], F32, name="acc%d" % half, bufs=2) for half in range(2)]
-            parts = [slice(half * BANK, (half + 1) * BANK) for half in range(2)]
+            if i == 0:
+                acc = [psum.tile([P, BANK], F32, name="acc%d" % half, bufs=2) for half in range(2)]
+                acc = acc + [psum.tile([P, BANK], F32, name="lead%d" % half) for half in range(2)]
+            elif i == 2:
+                acc = [psum.tile([P, BANK], F32, name="marks%d" % half) for half in range(2)]
+            else:
+                acc = [psum.tile([P, BANK], F32, name="acc%d" % half, bufs=2) for half in range(2)]
+            width = S // len(acc)
+            parts = [slice(half * width, (half + 1) * width) for half in range(len(acc))]
             for a in range(K_PASSES):
                 for half, part in enumerate(parts):
                     nc.tensor.matmul_mx(
-                        out=acc[half][:],
+                        out=acc[half][:, :width],
                         lhsT=w1_codes[g, a][:, cols].bitcast(E4M3),
                         lhsT_scale=w1_sc[g, a][:, cols],
                         rhs=v_codes[a][:, part].bitcast(E4M3),
@@ -154,96 +154,77 @@ def tile_list_skating_panel_median_kernel(
                     )
             banks[i] = acc
 
-        def empty_bank(i, half):
-            on_scalar = half == 0 and (i == 0 or i in SCALAR_TILES)
-            copy = nc.scalar.copy if on_scalar else nc.vector.tensor_copy
-            copy(h[i][:, half * BANK : (half + 1) * BANK], banks[i][half][:])
+        def empty_bank(i, half, copy):
+            width = S // len(banks[i])
+            copy(h[i][:, half * width : (half + 1) * width], banks[i][half][:, :width])
 
-        first, third, second, high, low, clipped, z = {}, {}, {}, {}, {}, {}, {}
-
-        def plane(tiles, i, cols):
-            g, t = divmod(i, PACK)
-            return tiles[g][:, t * PICKS + cols.start : t * PICKS + cols.stop]
-
-        def block(g):
-            return P if g == GROUPS - 1 else PICKS
-
-        def blocked(ap, g):
-            return ap.rearrange("p (b m) -> p b m", m=block(g))
-
-        def sorted_plane(tiles, i, cols):
-            g, t = divmod(i, PACK)
-            view = tiles[g][:].rearrange("p (b t m) -> p b t m", t=PACK, m=block(g))
-            return view[:, cols.start // block(g) : cols.stop // block(g), t]
+        def empty_on_vector(i):
+            for half in range(1 if i in SCALAR_TILES else 0, 2):
+                empty_bank(i, half, nc.vector.tensor_copy)
 
         def pick(dst, i, cols, judge):
             entries = picks[judge][:, cols.start // 16 : cols.stop // 16]
             nc.scalar.activation(dst, h[i][:].indirect(entries), SIGMOID)
 
-        def look_up(i, cols):
-            g, t = divmod(i, PACK)
-            if t == 0:
-                first[g] = ring.tile([P, PACK * PICKS], F32, name="first")
-                third[g] = ring.tile([P, PACK * PICKS], F32, name="third")
-            second[i, cols.start] = keep.tile(
-                [P, cols.stop - cols.start], F32, name="second%d_%d" % (i, cols.start)
-            )
-            pick(second[i, cols.start][:], i, cols, 0)
-            pick(plane(first, i, cols), i, cols, 1)
-            if cols.start == 0 or i < TILES - 2:
-                pick(plane(third, i, cols), i, cols, 2)
-
         def gain_of(i):
             g, t = divmod(i, PACK)
             return gains[:, g, t : t + 1]
 
-        weighed = {}
+        whole = slice(0, PICKS)
+        lone, first, third, weighed, high, mate, minima, z = {}, {}, {}, {}, {}, {}, {}, {}
 
-        def weigh_second(i, cols, beside_copies=False):
-            b = second[i, cols.start][:]
-            if beside_copies:
-                scaled = keep.tile([P, cols.stop - cols.start], F32, name="scaled")
-                nc.gpsimd.tensor_scalar(scaled[:], b, gain_of(i), 0.0, ALU.mult, ALU.add)
-                weighed[i, cols.start] = scaled[:]
-            else:
-                nc.vector.tensor_scalar(b, b, gain_of(i), None, ALU.mult)
-                weighed[i, cols.start] = b
+        def look_up(i):
+            lone[i] = ring.tile([P, PICKS], F32, name="lone", bufs=3)
+            first[i] = ring.tile([P, PICKS], F32, name="first", bufs=3)
+            third[i] = ring.tile([P, PICKS], F32, name="third", bufs=3)
+            pick(lone[i][:], i, whole, 0)
+            pick(first[i][:], i, whole, 1)
+            pick(third[i][:], i, whole, 2)
 
-        def upper(i, cols):
-            high[i] = ring.tile([P, cols.stop - cols.start], F32, name="high")
-            a, b = plane(first, i, cols), weighed[i, cols.start]
-            nc.vector.scalar_tensor_tensor(high[i][:], a, gain_of(i), b, ALU.mult, ALU.max)
+        def weigh(i):
+            weighed[i] = keep.tile([P, PICKS], F32, name="weighed", align_bytes=64)
+            nc.gpsimd.tensor_scalar(weighed[i][:], lone[i][:], gain_of(i), 0.0, ALU.mult, ALU.add)
 
-        def lower(i, cols):
+        def upper(i):
+            high[i] = ring.tile([P, PICKS], F32, name="high")
+            nc.vector.scalar_tensor_tensor(high[i][:], first[i][:], gain_of(i), weighed[i][:], ALU.mult, ALU.max)
+
+        def block(g):
+            return SIDE if g == GROUPS - 1 else PICKS
+
+        def minima_of(g):
+            if g not in minima:
+                minima[g] = ring.tile([P, 2, PACK * PICKS], F32, name="minima")
+            return minima[g]
+
+        def minimum(i, which, picked, bound):
             g, t = divmod(i, PACK)
-            if t == 0:
-                low[g] = ring.tile([P, PACK * PICKS], F32, name="low")
-                clipped[g] = ring.tile([P, PACK * PICKS], F32, name="clipped")
-            a, b = blocked(plane(first, i, cols), g), blocked(weighed[i, cols.start], g)
-            nc.vector.scalar_tensor_tensor(sorted_plane(low, i, cols), a, gain_of(i), b, ALU.mult, ALU.min)
+            m = block(g)
+            dst = minima_of(g)[:, which].rearrange("p (b t m) -> p b t m", t=PACK, m=m)[:, :, t]
+            nc.vector.scalar_tensor_tensor(
+                dst,
+                picked[:].rearrange("p (b m) -> p b m", m=m),
+                gain_of(i),
+                bound[:].rearrange("p (b m) -> p b m", m=m),
+                ALU.mult,
+                ALU.min,
+            )
 
-        def clip_third(i, cols):
-            g = i // PACK
-            c = blocked(plane(third, i, cols), g)
-            origin = cols.start // SIDE * SIDE
-            bound = blocked(high[i][:, cols.start - origin : cols.stop - origin], g)
-            nc.vector.scalar_tensor_tensor(sorted_plane(clipped, i, cols), c, gain_of(i), bound, ALU.mult, ALU.min)
-
-        z_codes = [keep.tile([P, PICKS], U32, name="z_codes%d" % g, align_bytes=64) for g in range(GROUPS)]
+        z_codes = {g: keep.tile([P, PICKS], U32, name="z_codes%d" % g, align_bytes=64) for g in (0, 2)}
         z_sc = [keep.tile([P, PICKS], U8, name="z_sc%d" % g, align_bytes=64) for g in range(GROUPS)]
         marks = {}
 
         def median(g, part):
             z[g, part.start] = ring.tile([P, part.stop - part.start, PACK], BF16, name="z", align_bytes=64)
-            for c0 in range(part.start, part.stop, block(g)):
-                span = slice(PACK * c0, PACK * (c0 + block(g)))
-                dst = z[g, part.start][:, c0 - part.start : c0 - part.start + block(g)]
-                nc.vector.tensor_tensor(
-                    dst.rearrange("p (c i) t -> p c t i", i=4),
-                    low[g][:, span].rearrange("p (t c i) -> p c t i", t=PACK, i=4),
-                    clipped[g][:, span].rearrange("p (t c i) -> p c t i", t=PACK, i=4),
-                    ALU.max,
-                )
+            b, c0 = divmod(part.start, block(g))
+            view = minima[g][:].rearrange("p s (b t m) -> p s b t m", t=PACK, m=block(g))
+            low, clipped = [view[:, s, b, :, c0 : c0 + part.stop - part.start] for s in range(2)]
+            nc.vector.tensor_tensor(
+                z[g, part.start][:].rearrange("p (c i) t -> p c t i", i=4),
+                low.rearrange("p t (c i) -> p c t i", i=4),
+                clipped.rearrange("p t (c i) -> p c t i", i=4),
+                ALU.max,
+            )
 
         def quantise_z(g, part):
             nc.vector.quantize_mx(
@@ -252,137 +233,190 @@ def tile_list_skating_panel_median_kernel(
                 in_=z[g, part.start][:].rearrange("p m t -> p (m t)"),
             )
 
-        whole = slice(0, PICKS)
         sides = [slice(0, SIDE), slice(SIDE, SIDE + P), slice(SIDE + P, PICKS)]
-        steps = [(i, whole) for i in range(TILES - 2)]
-        steps = steps + [(i, cols) for cols in (sides[0], slice(SIDE, PICKS)) for i in (TILES - 2, TILES - 1)]
 
-        def blocks_of(side):
-            return [(n, c) for c in range(side.start, side.stop, P) for n in range(N // P)]
-
-        def place(side, n, c):
-            if side.start == 0:
-                return n, c // P
-            return n // 2, n % 2
+        def shared(side):
+            return 1 if side.stop == PICKS else 2
 
         def second_product(g, side):
-            for n, c in blocks_of(side):
-                bank, slot = place(side, n, c)
+            width = side.stop - side.start
+            for n in range(N // P):
+                bank, slot = divmod(n, shared(side))
                 if g == 0 and slot == 0:
                     if side.start == 0:
                         marks[side.start, bank] = psum.tile([P, BANK], F32, name="marks%d" % bank)
+                    elif bank >= 2:
+                        marks[side.start, bank] = psum.tile([P, BANK], F32, name="lead%d" % (bank - 2))
                     else:
                         marks[side.start, bank] = psum.tile([P, BANK], F32, name="acc%d" % bank, bufs=2)
                 nc.tensor.matmul_mx(
-                    out=marks[side.start, bank][:, slot * P : (slot + 1) * P],
+                    out=marks[side.start, bank][:, slot * width : (slot + 1) * width],
                     lhsT=w2_codes[:, g, 2 * P * n : 2 * P * (n + 1)].bitcast(E2M1),
                     lhsT_scale=w2_sc[:, g, P * n : P * (n + 1)],
-                    rhs=z_codes[g][:, c : c + P].bitcast(E4M3),
-                    rhs_scale=z_sc[g][:, c : c + P],
+                    rhs=z_codes[g][:, side].bitcast(E4M3),
+                    rhs_scale=z_sc[g][:, side],
                     start=(g == 0 and slot == 0),
-                    stop=(g == GROUPS - 1 and slot == 1),
+                    stop=(g == GROUPS - 1 and slot == shared(side) - 1),
                 )
 
         def store(side):
-            for bank in range(N // P if side.start == 0 else 2):
-                result = ring.tile([P, SIDE], F32, name="result", bufs=8)
-                last = side.stop == PICKS and bank == 1
-                copy = nc.vector.tensor_copy if last else nc.scalar.copy
-                copy(result[:], marks[side.start, bank][:, :SIDE])
-                if side.start == 0:
-                    nc.sync.dma_start(out=out[bank * P : (bank + 1) * P, side], in_=result[:])
+            width = side.stop - side.start
+            for pair in range(2):
+                result = keep.tile([P, 2 * width], F32, name="result%d%d" % (side.start, pair))
+                if shared(side) == 2:
+                    nc.scalar.copy(result[:], marks[side.start, pair][:, : 2 * width])
                 else:
-                    rows = out[2 * bank * P : 2 * (bank + 1) * P, side]
-                    nc.sync.dma_start(
-                        out=rows.rearrange("(n p) m -> p n m", p=P),
-                        in_=result[:].rearrange("p (n m) -> p n m", n=2),
-                    )
+                    nc.scalar.copy(result[:, :width], marks[side.start, 2 * pair][:, :width])
+                    nc.vector.tensor_copy(result[:, width:], marks[side.start, 2 * pair + 1][:, :width])
+                rows = out[2 * pair * P : 2 * (pair + 1) * P, side]
+                nc.sync.dma_start(
+                    out=rows.rearrange("(n p) m -> p n m", p=P),
+                    in_=result[:].rearrange("p (n m) -> p n m", n=2),
+                )
 
-        for pair in range(2):
-            round_w1(0, 0, pair, nc.scalar.copy)
-        round_w1(0, 1, 0, nc.scalar.copy, by_piece=True)
-        round_w1(0, 1, 1, nc.scalar.copy)
+        nc.vector.tensor_copy(v_sc[:], table_sc[:].indirect(idx[:]))
+        nc.vector.tensor_copy(v_codes[0][:], table[0][:].bitcast(U32).indirect(idx[:]))
+        for u in range(2):
+            for pair in range(2):
+                round_lead(0, pair, u)
         quantise_w1(0, 0, 0, 2)
-        quantise_w1(0, 1, 0, 1)
-        first_product(0)
-        for half in range(2):
-            empty_bank(0, half)
-        quantise_w1(0, 1, 1, 2)
-        first_product(1)
-        for half in range(2):
-            empty_bank(1, half)
         quantise_w1(0, 0, 2, 4)
+        nc.vector.tensor_copy(v_codes[1][:], table[1][:].bitcast(U32).indirect(idx[:]))
+        for u in range(2):
+            round_lead(1, 0, u)
+        round_lead(1, 1)
+        quantise_w1(0, 1, 0, 1)
+        quantise_w1(0, 1, 1, 2)
+        first_product(0)
+        for quarter in range(4):
+            empty_bank(0, quarter, nc.vector.tensor_copy if quarter % 2 else nc.scalar.copy)
+        first_product(1)
         quantise_w1(0, 1, 2, 4)
+        empty_on_vector(1)
         first_product(2)
-        look_up(*steps[0])
-        weigh_second(*steps[0], beside_copies=True)
+        look_up(0)
+        weigh(0)
+        empty_on_vector(2)
         round_whole(1, 0)
-        for half in range(2):
-            empty_bank(2, half)
-        quantise_w1(1, 0, 0, PACK)
         round_whole(1, 1)
-        waiting = (1, 1)
-        finished = closed = None
-        for step, (i, cols) in enumerate(steps):
-            g, t = divmod(i, PACK)
-            ahead = steps[step + 1] if step + 1 < len(steps) else None
-            coming = step + AHEAD
-            beside_copies = coming < TILES
-            closes = g > 0 and t == 0
+
+        fillers = {
+            0: [lambda: quantise_w1(1, 0)],
+            3: [lambda: quantise_w1(2, 0)],
+            4: [lambda: quantise_w1(2, 1)],
+            5: [lambda: quantise_z(0, whole), lambda: second_product(0, sides[0])],
+        }
+        extras = {
+            0: [lambda: quantise_w1(1, 1)],
+            2: [lambda: round_whole(2, 0)],
+            3: [lambda: round_whole(2, 1)],
+            4: [lambda: median(0, whole)],
+            7: [lambda: median(1, whole)],
+        }
+
+        last = GROUPS - 1
+        halves = [sides[0], slice(SIDE, PICKS)]
+        late = [(i, b) for b in range(2) for i in (TILES - 2, TILES - 1)]
+        trio = {}
+
+        def late_planes(i, b):
+            view = minima_of(last)[:].rearrange("p s (b t m) -> p s b t m", t=PACK, m=SIDE)
+            return view[:, :, b, i % PACK]
+
+        def look_up_late(i, b):
+            trio[i, b] = ring.tile([P, 3, SIDE], F32, name="third", bufs=3)
+            pick(trio[i, b][:, 2], i, halves[b], 0)
+            pick(trio[i, b][:, 0], i, halves[b], 1)
+            pick(trio[i, b][:, 1], i, halves[b], 2)
+
+        def weigh_late(i, b):
+            if (i, b) == late[3]:
+                mate[i, b] = minima[last][:, 0, : 2 * SIDE].rearrange("p (s m) -> p s m", s=2)
+            elif (i, b) == late[0]:
+                mate[i, b] = first[WHOLE_TILES - 1][:].rearrange("p (s m) -> p s m", s=2)
+            else:
+                mate[i, b] = z[1, 0][:].rearrange("p m t -> p (m t)").bitcast(F32)[:, : 2 * SIDE]
+                mate[i, b] = mate[i, b].rearrange("p (s m) -> p s m", s=2)
+            nc.vector.tensor_scalar(mate[i, b][:, 0], trio[i, b][:, 2], gain_of(i), None, ALU.mult)
+
+        def upper_late(i, b):
+            nc.vector.scalar_tensor_tensor(
+                mate[i, b][:, 1], trio[i, b][:, 0], gain_of(i), mate[i, b][:, 0], ALU.mult, ALU.max
+            )
+
+        def minima_late(i, b, cols=slice(0, SIDE), which=slice(0, 2)):
+            nc.vector.scalar_tensor_tensor(
+                late_planes(i, b)[:, which, cols],
+                trio[i, b][:, which, cols],
+                gain_of(i),
+                mate[i, b][:, which, cols],
+                ALU.mult,
+                ALU.min,
+            )
+
+        for i in range(WHOLE_TILES):
+            coming = i + AHEAD
             if coming < TILES:
                 first_product(coming)
-            if step + 2 in SCALAR_TILES:
-                empty_bank(step + 2, 0)
-            if ahead:
-                look_up(*ahead)
-            if finished:
-                median(*finished)
-            upper(i, cols)
-            if waiting:
-                quantise_w1(*waiting, 0, PACK)
-            if closed is not None:
-                quantise_z(closed, whole)
-                second_product(closed, sides[0])
-            if finished:
-                quantise_z(*finished)
-                second_product(*finished)
-                store(finished[1])
-            lower(i, cols)
-            if beside_copies:
-                weigh_second(*ahead, beside_copies=True)
-                clip_third(i, cols)
-                for half in range(1 if coming in SCALAR_TILES else 0, 2):
-                    empty_bank(coming, half)
-            if ahead and i == TILES - 1:
-                clip_third(i, cols)
-            if closes:
-                median(g - 1, whole)
-            if ahead and not beside_copies:
-                weigh_second(*ahead)
-            waiting = (GROUPS - 1, step - 2) if step in (2, 3) else None
-            if waiting:
-                round_whole(*waiting)
-            if step == TILES - 2:
-                for side in sides[1:]:
-                    for earlier in range(GROUPS - 1):
-                        second_product(earlier, side)
-            if not beside_copies and (i < TILES - 2 or (i < TILES - 1 and cols.start == 0)):
-                clip_third(i, cols)
-            closed = g - 1 if closes else None
-            finished = (g, cols) if i == TILES - 1 else None
-        last = GROUPS - 1
+            if i + 2 in SCALAR_TILES:
+                empty_bank(i + 2, 0, nc.scalar.copy)
+            if i + 1 < WHOLE_TILES:
+                look_up(i + 1)
+            else:
+                look_up_late(*late[0])
+            upper(i)
+            for filler in fillers.get(i, []):
+                filler()
+            minimum(i, 0, first[i], weighed[i])
+            if i + 1 < WHOLE_TILES:
+                weigh(i + 1)
+            minimum(i, 1, third[i], high[i])
+            if coming < TILES:
+                empty_on_vector(coming)
+            for extra in extras.get(i, []):
+                extra()
+
+        look_up_late(*late[1])
+        both = ring.tile([P, 2, 3, SIDE], F32, name="third", bufs=3)
+        trio[late[2]], trio[late[3]] = both[:, 0], both[:, 1]
+        for i, b in late[2:]:
+            for place, judge in ((2, 0), (0, 1)):
+                pick(trio[i, b][:, place], i, halves[b], judge)
+        quarters = [slice(0, P), slice(P, SIDE)]
+        for side, cols in zip(sides[1:], quarters):
+            for i, b in late[2:]:
+                pick(trio[i, b][:, 1, cols], i, side, 2)
+        weigh_late(*late[0])
+        z_codes[1] = keep.tile([P, PICKS], U32, name="weighed", align_bytes=64)
+        quantise_z(1, whole)
+        second_product(1, sides[0])
         for side in sides[1:]:
-            for i in (TILES - 2, TILES - 1):
-                pick(plane(third, i, side), i, side, 2)
-        clip_third(TILES - 2, sides[1])
-        clip_third(TILES - 1, sides[1])
-        clip_third(TILES - 2, sides[2])
+            for earlier in range(last):
+                second_product(earlier, side)
+        upper_late(*late[0])
+        minima_late(*late[0], which=slice(0, 1))
+        weigh_late(*late[1])
+        minima_late(*late[0], which=slice(1, 2))
+        upper_late(*late[1])
+        minima_late(*late[1], which=slice(0, 1))
+        minima_late(*late[1], which=slice(1, 2))
+        weigh_late(*late[2])
+        median(last, sides[0])
+        upper_late(*late[2])
+        weigh_late(*late[3])
+        quantise_z(last, sides[0])
+        second_product(last, sides[0])
+        store(sides[0])
+        upper_late(*late[3])
+        minima_late(*late[2], quarters[0])
+        minima_late(*late[3], quarters[0])
+        minima_late(*late[2], quarters[1])
         median(last, sides[1])
-        clip_third(TILES - 1, sides[2])
+        minima_late(*late[3], quarters[1])
         quantise_z(last, sides[1])
         second_product(last, sides[1])
-        store(sides[1])
         median(last, sides[2])
         quantise_z(last, sides[2])
         second_product(last, sides[2])
-        store(sides[2])
+        for side in sides[1:]:
+            store(side)

@@ -27,6 +27,7 @@ WHOLE_TILES = TILES - 2
 SIDE = PICKS // 2
 SCALAR_TILES = (6, 7, 9, 10, 11)
 AHEAD = 3
+SHARE = 32
 
 
 def tile_list_skating_panel_median_kernel(
@@ -67,8 +68,8 @@ def tile_list_skating_panel_median_kernel(
                 out=table[a][:], in_=tab_words[a].rearrange("p n t -> p (n t)").bitcast(I32)
             )
 
-        nc.sync.dma_start(idx[:], offs)
         load_w1(0, 0, 0, 2)
+        nc.sync.dma_start(idx[:], offs)
         nc.sync.dma_start(picks[0][:], pos1)
         for q in range(4):
             nc.sync.dma_start(
@@ -100,7 +101,7 @@ def tile_list_skating_panel_median_kernel(
 
         w1_codes, w1_sc, rounded = {}, {}, {}
 
-        def round_lead(a, pair, u=None):
+        def round_lead(a, pair, u=None, part=slice(0, P // 2), copy=nc.scalar.copy):
             if (0, a) not in rounded:
                 rounded[0, a] = ring.tile([P, PACK, P, PACK], BF16, name="rounded", bufs=4, align_bytes=64)
             ts = slice(2 * pair, 2 * pair + 2)
@@ -109,7 +110,7 @@ def tile_list_skating_panel_median_kernel(
             if u is None:
                 nc.scalar.copy(dst, src)
             else:
-                nc.scalar.copy(dst[:, u], src[:, u])
+                copy(dst[:, u, part], src[:, u, part])
 
         def round_whole(g, a):
             rounded[g, a] = ring.tile([P, PACK, P, PACK], BF16, name="rounded", bufs=4, align_bytes=64)
@@ -282,9 +283,11 @@ def tile_list_skating_panel_median_kernel(
         quantise_w1(0, 0, 0, 2)
         quantise_w1(0, 0, 2, 4)
         nc.vector.tensor_copy(v_codes[1][:], table[1][:].bitcast(U32).indirect(idx[:]))
-        for u in range(2):
-            round_lead(1, 0, u)
-        round_lead(1, 1)
+        round_lead(1, 0, 0)
+        round_lead(1, 1, 0)
+        round_lead(1, 0, 1, slice(0, SHARE), nc.vector.tensor_copy)
+        round_lead(1, 0, 1, slice(SHARE, P // 2))
+        round_lead(1, 1, 1)
         quantise_w1(0, 1, 0, 1)
         quantise_w1(0, 1, 1, 2)
         first_product(0)

from contextlib import ExitStack

import concourse.mybir as mybir

K, T, S, PICKS, H, N = 1024, 2048, 1024, 512, 1536, 512
FLOPS = 2 * K * H * S + 2 * H * N * PICKS

F32 = mybir.dt.float32
BF16 = mybir.dt.bfloat16
I32 = mybir.dt.int32
U32 = mybir.dt.uint32
U16 = mybir.dt.uint16
U8 = mybir.dt.uint8
E4M3 = mybir.dt.float8_e4m3fn_x4
E2M1 = mybir.dt.float4_e2m1fn_x4
ALU = mybir.AluOpType
SIGMOID = mybir.ActivationFunctionType.Sigmoid

P = 128
PACK = 4
PASS = P * PACK
BANK = 512
K_PASSES = K // PASS
GROUPS = H // PASS
TILES = GROUPS * PACK
WHOLE_TILES = TILES - 2
SIDE = PICKS // 2
SCALAR_TILES = (6, 7, 9, 10, 11)
AHEAD = 3
SHARE = 32


def tile_list_skating_panel_median_kernel(
    tc, tab_words, tab_scales, offs, w1, pos1, pos2, pos3, gain, w2_words, w2_scales, out
):
    nc = tc.nc
    with ExitStack() as ctx:
        keep = ctx.enter_context(tc.tile_pool(name="keep", bufs=1))
        ring = ctx.enter_context(tc.tile_pool(name="ring", bufs=2))
        psum = ctx.enter_context(tc.psum_pool(name="psum", bufs=1))

        idx = keep.tile([P, S // 16], U16, name="idx")
        picks = [keep.tile([P, PICKS // 16], U16, name="pick%d" % i) for i in range(3)]
        table = [keep.tile([P, T], I32, name="table%d" % a) for a in range(K_PASSES)]
        table_sc = keep.tile([P, T], U8, name="table_sc")
        gains = keep.tile([P, GROUPS, PACK], F32, name="gains")
        w2_codes = keep.tile([P, GROUPS, 2 * N], U8, name="w2_codes", align_bytes=64)
        w2_sc = keep.tile([P, GROUPS, N], U8, name="w2_sc", align_bytes=64)
        warm = keep.tile([P, 8], F32, name="warm")

        nc.gpsimd.memset(table_sc[:].bitcast(I32), 0)
        nc.vector.memset(warm[:], 0.0)
        nc.scalar.activation(warm[:, 0:1], warm[:, 1:2], SIGMOID)
        nc.vector.memset(w2_sc[:].bitcast(I32), 0)

        raw = {}

        def load_w1(g, a, u=0, n=1):
            width = PASS // n
            if u == 0:
                raw[g, a] = keep.tile([P, n, PACK, width], F32, name="raw%d%d" % (g, a))
            c0 = g * PASS + u * width
            rows = w1[a * PASS : (a + 1) * PASS, c0 : c0 + width]
            nc.sync.dma_start(out=raw[g, a][:, u], in_=rows.rearrange("(p j) c -> p j c", j=PACK))

        def load_table(a):
            nc.sync.dma_start(
                out=table[a][:], in_=tab_words[a].rearrange("p n t -> p (n t)").bitcast(I32)
            )

        load_w1(0, 0, 0, 2)
        nc.sync.dma_start(idx[:], offs)
        nc.sync.dma_start(picks[0][:], pos1)
        for q in range(4):
            nc.sync.dma_start(
                out=table_sc[32 * q : 32 * q + 4 * K_PASSES, :].bitcast(I32),
                in_=tab_scales[:, 4 * q : 4 * q + 4, :].bitcast(I32),
            )
        load_table(0)
        load_w1(0, 0, 1, 2)
        load_table(1)
        load_w1(0, 1, 0, 2)
        load_w1(0, 1, 1, 2)
        nc.sync.dma_start(picks[1][:], pos2)
        nc.sync.dma_start(picks[2][:], pos3)
        nc.sync.dma_start(out=gains[:], in_=gain.rearrange("(g p t) -> p g t", p=P, t=PACK))
        for g in range(1, GROUPS):
            for a in range(K_PASSES):
                load_w1(g, a)
        nc.sync.dma_start(
            out=w2_codes[:].bitcast(I32), in_=w2_words.rearrange("g p c -> p g c").bitcast(I32)
        )
        for q in range(4):
            nc.sync.dma_start(
                out=w2_sc[32 * q : 32 * q + 4, :, :].bitcast(I32),
                in_=w2_scales[:, 4 * q : 4 * q + 4, :].rearrange("g r c -> r g c").bitcast(I32),
            )

        v_codes = [keep.tile([P, S], U32, name="v_codes%d" % a, align_bytes=64) for a in range(K_PASSES)]
        v_sc = keep.tile([P, S], U8, name="v_sc", align_bytes=64)

        w1_codes, w1_sc, rounded = {}, {}, {}

        def round_lead(a, pair, u=None, part=slice(0, P // 2), copy=nc.scalar.copy):
            if (0, a) not in rounded:
                rounded[0, a] = ring.tile([P, PACK, P, PACK], BF16, name="rounded", bufs=4, align_bytes=64)
            ts = slice(2 * pair, 2 * pair + 2)
            dst = rounded[0, a][:, ts].rearrange("p t (u m) j -> p u m j t", u=2)
            src = raw[0, a][:].rearrange("p u j (m t) -> p u m j t", t=PACK)[:, :, :, :, ts]
            if u is None:
                nc.scalar.copy(dst, src)
            else:
                copy(dst[:, u, part], src[:, u, part])

        def round_whole(g, a):
            rounded[g, a] = ring.tile([P, PACK, P, PACK], BF16, name="rounded", bufs=4, align_bytes=64)
            dst = rounded[g, a][:].rearrange("p t m j -> p m j t")
            nc.vector.tensor_copy(dst, raw[g, a][:, 0].rearrange("p j (m t) -> p m j t", t=PACK))

        def quantise_w1(g, a, t0=0, t1=PACK):
            if t0 == 0:
                w1_codes[g, a] = keep.tile([P, PASS], U32, name="w1_codes%d%d" % (g, a), align_bytes=64)
                w1_sc[g, a] = keep.tile([P, PASS], U8, name="w1_sc%d%d" % (g, a), align_bytes=64)
            nc.vector.quantize_mx(
                out=w1_codes[g, a][:, t0 * P : t1 * P].bitcast(E4M3),
                scales=w1_sc[g, a][:, t0 * P : t1 * P],
                in_=rounded[g, a][:, t0:t1].rearrange("p t m j -> p (t m j)"),
            )

        h, banks = {}, {}

        def first_product(i):
            g, t = divmod(i, PACK)
            cols = slice(t * P, (t + 1) * P)
            h[i] = ring.tile([P, S], F32, name="h", bufs=AHEAD + 1)
            if i == 0:
                acc = [psum.tile([P, BANK], F32, name="acc%d" % half, bufs=2) for half in range(2)]
                acc = acc + [psum.tile([P, BANK], F32, name="lead%d" % half) for half in range(2)]
            elif i == 2:
                acc = [psum.tile([P, BANK], F32, name="marks%d" % half) for half in range(2)]
            else:
                acc = [psum.tile([P, BANK], F32, name="acc%d" % half, bufs=2) for half in range(2)]
            width = S // len(acc)
            parts = [slice(half * width, (half + 1) * width) for half in range(len(acc))]
            for a in range(K_PASSES):
                for half, part in enumerate(parts):
                    nc.tensor.matmul_mx(
                        out=acc[half][:, :width],
                        lhsT=w1_codes[g, a][:, cols].bitcast(E4M3),
                        lhsT_scale=w1_sc[g, a][:, cols],
                        rhs=v_codes[a][:, part].bitcast(E4M3),
                        rhs_scale=v_sc[4 * a :, part],
                        start=(a == 0),
                        stop=(a == K_PASSES - 1),
                    )
            banks[i] = acc

        def empty_bank(i, half, copy):
            width = S // len(banks[i])
            copy(h[i][:, half * width : (half + 1) * width], banks[i][half][:, :width])

        def empty_on_vector(i):
            for half in range(1 if i in SCALAR_TILES else 0, 2):
                empty_bank(i, half, nc.vector.tensor_copy)

        def pick(dst, i, cols, judge):
            entries = picks[judge][:, cols.start // 16 : cols.stop // 16]
            nc.scalar.activation(dst, h[i][:].indirect(entries), SIGMOID)

        def gain_of(i):
            g, t = divmod(i, PACK)
            return gains[:, g, t : t + 1]

        whole = slice(0, PICKS)
        lone, first, third, weighed, high, mate, minima, z = {}, {}, {}, {}, {}, {}, {}, {}

        def look_up(i):
            lone[i] = ring.tile([P, PICKS], F32, name="lone", bufs=3)
            first[i] = ring.tile([P, PICKS], F32, name="first", bufs=3)
            third[i] = ring.tile([P, PICKS], F32, name="third", bufs=3)
            pick(lone[i][:], i, whole, 0)
            pick(first[i][:], i, whole, 1)
            pick(third[i][:], i, whole, 2)

        def weigh(i):
            weighed[i] = keep.tile([P, PICKS], F32, name="weighed", align_bytes=64)
            nc.gpsimd.tensor_scalar(weighed[i][:], lone[i][:], gain_of(i), 0.0, ALU.mult, ALU.add)

        def upper(i):
            high[i] = ring.tile([P, PICKS], F32, name="high")
            nc.vector.scalar_tensor_tensor(high[i][:], first[i][:], gain_of(i), weighed[i][:], ALU.mult, ALU.max)

        def block(g):
            return SIDE if g == GROUPS - 1 else PICKS

        def minima_of(g):
            if g not in minima:
                minima[g] = ring.tile([P, 2, PACK * PICKS], F32, name="minima")
            return minima[g]

        def minimum(i, which, picked, bound):
            g, t = divmod(i, PACK)
            m = block(g)
            dst = minima_of(g)[:, which].rearrange("p (b t m) -> p b t m", t=PACK, m=m)[:, :, t]
            nc.vector.scalar_tensor_tensor(
                dst,
                picked[:].rearrange("p (b m) -> p b m", m=m),
                gain_of(i),
                bound[:].rearrange("p (b m) -> p b m", m=m),
                ALU.mult,
                ALU.min,
            )

        z_codes = {g: keep.tile([P, PICKS], U32, name="z_codes%d" % g, align_bytes=64) for g in (0, 2)}
        z_sc = [keep.tile([P, PICKS], U8, name="z_sc%d" % g, align_bytes=64) for g in range(GROUPS)]
        marks = {}

        def median(g, part):
            z[g, part.start] = ring.tile([P, part.stop - part.start, PACK], BF16, name="z", align_bytes=64)
            b, c0 = divmod(part.start, block(g))
            view = minima[g][:].rearrange("p s (b t m) -> p s b t m", t=PACK, m=block(g))
            low, clipped = [view[:, s, b, :, c0 : c0 + part.stop - part.start] for s in range(2)]
            nc.vector.tensor_tensor(
                z[g, part.start][:].rearrange("p (c i) t -> p c t i", i=4),
                low.rearrange("p t (c i) -> p c t i", i=4),
                clipped.rearrange("p t (c i) -> p c t i", i=4),
                ALU.max,
            )

        def quantise_z(g, part):
            nc.vector.quantize_mx(
                out=z_codes[g][:, part].bitcast(E4M3),
                scales=z_sc[g][:, part],
                in_=z[g, part.start][:].rearrange("p m t -> p (m t)"),
            )

        sides = [slice(0, SIDE), slice(SIDE, SIDE + P), slice(SIDE + P, PICKS)]

        def shared(side):
            return 1 if side.stop == PICKS else 2

        def second_product(g, side):
            width = side.stop - side.start
            for n in range(N // P):
                bank, slot = divmod(n, shared(side))
                if g == 0 and slot == 0:
                    if side.start == 0:
                        marks[side.start, bank] = psum.tile([P, BANK], F32, name="marks%d" % bank)
                    elif bank >= 2:
                        marks[side.start, bank] = psum.tile([P, BANK], F32, name="lead%d" % (bank - 2))
                    else:
                        marks[side.start, bank] = psum.tile([P, BANK], F32, name="acc%d" % bank, bufs=2)
                nc.tensor.matmul_mx(
                    out=marks[side.start, bank][:, slot * width : (slot + 1) * width],
                    lhsT=w2_codes[:, g, 2 * P * n : 2 * P * (n + 1)].bitcast(E2M1),
                    lhsT_scale=w2_sc[:, g, P * n : P * (n + 1)],
                    rhs=z_codes[g][:, side].bitcast(E4M3),
                    rhs_scale=z_sc[g][:, side],
                    start=(g == 0 and slot == 0),
                    stop=(g == GROUPS - 1 and slot == shared(side) - 1),
                )

        def store(side):
            width = side.stop - side.start
            for pair in range(2):
                result = keep.tile([P, 2 * width], F32, name="result%d%d" % (side.start, pair))
                if shared(side) == 2:
                    nc.scalar.copy(result[:], marks[side.start, pair][:, : 2 * width])
                else:
                    nc.scalar.copy(result[:, :width], marks[side.start, 2 * pair][:, :width])
                    nc.vector.tensor_copy(result[:, width:], marks[side.start, 2 * pair + 1][:, :width])
                rows = out[2 * pair * P : 2 * (pair + 1) * P, side]
                nc.sync.dma_start(
                    out=rows.rearrange("(n p) m -> p n m", p=P),
                    in_=result[:].rearrange("p (n m) -> p n m", n=2),
                )

        nc.vector.tensor_copy(v_sc[:], table_sc[:].indirect(idx[:]))
        nc.vector.tensor_copy(v_codes[0][:], table[0][:].bitcast(U32).indirect(idx[:]))
        for u in range(2):
            for pair in range(2):
                round_lead(0, pair, u)
        quantise_w1(0, 0, 0, 2)
        quantise_w1(0, 0, 2, 4)
        nc.vector.tensor_copy(v_codes[1][:], table[1][:].bitcast(U32).indirect(idx[:]))
        round_lead(1, 0, 0)
        round_lead(1, 1, 0)
        round_lead(1, 0, 1, slice(0, SHARE), nc.vector.tensor_copy)
        round_lead(1, 0, 1, slice(SHARE, P // 2))
        round_lead(1, 1, 1)
        quantise_w1(0, 1, 0, 1)
        quantise_w1(0, 1, 1, 2)
        first_product(0)
        for quarter in range(4):
            empty_bank(0, quarter, nc.vector.tensor_copy if quarter % 2 else nc.scalar.copy)
        first_product(1)
        quantise_w1(0, 1, 2, 4)
        empty_on_vector(1)
        first_product(2)
        look_up(0)
        weigh(0)
        empty_on_vector(2)
        round_whole(1, 0)
        round_whole(1, 1)

        fillers = {
            0: [lambda: quantise_w1(1, 0)],
            3: [lambda: quantise_w1(2, 0)],
            4: [lambda: quantise_w1(2, 1)],
            5: [lambda: quantise_z(0, whole), lambda: second_product(0, sides[0])],
        }
        extras = {
            0: [lambda: quantise_w1(1, 1)],
            2: [lambda: round_whole(2, 0)],
            3: [lambda: round_whole(2, 1)],
            4: [lambda: median(0, whole)],
            7: [lambda: median(1, whole)],
        }

        last = GROUPS - 1
        halves = [sides[0], slice(SIDE, PICKS)]
        late = [(i, b) for b in range(2) for i in (TILES - 2, TILES - 1)]
        trio = {}

        def late_planes(i, b):
            view = minima_of(last)[:].rearrange("p s (b t m) -> p s b t m", t=PACK, m=SIDE)
            return view[:, :, b, i % PACK]

        def look_up_late(i, b):
            trio[i, b] = ring.tile([P, 3, SIDE], F32, name="third", bufs=3)
            pick(trio[i, b][:, 2], i, halves[b], 0)
            pick(trio[i, b][:, 0], i, halves[b], 1)
            pick(trio[i, b][:, 1], i, halves[b], 2)

        def weigh_late(i, b):
            if (i, b) == late[3]:
                mate[i, b] = minima[last][:, 0, : 2 * SIDE].rearrange("p (s m) -> p s m", s=2)
            elif (i, b) == late[0]:
                mate[i, b] = first[WHOLE_TILES - 1][:].rearrange("p (s m) -> p s m", s=2)
            else:
                mate[i, b] = z[1, 0][:].rearrange("p m t -> p (m t)").bitcast(F32)[:, : 2 * SIDE]
                mate[i, b] = mate[i, b].rearrange("p (s m) -> p s m", s=2)
            nc.vector.tensor_scalar(mate[i, b][:, 0], trio[i, b][:, 2], gain_of(i), None, ALU.mult)

        def upper_late(i, b):
            nc.vector.scalar_tensor_tensor(
                mate[i, b][:, 1], trio[i, b][:, 0], gain_of(i), mate[i, b][:, 0], ALU.mult, ALU.max
            )

        def minima_late(i, b, cols=slice(0, SIDE), which=slice(0, 2)):
            nc.vector.scalar_tensor_tensor(
                late_planes(i, b)[:, which, cols],
                trio[i, b][:, which, cols],
                gain_of(i),
                mate[i, b][:, which, cols],
                ALU.mult,
                ALU.min,
            )

        for i in range(WHOLE_TILES):
            coming = i + AHEAD
            if coming < TILES:
                first_product(coming)
            if i + 2 in SCALAR_TILES:
                empty_bank(i + 2, 0, nc.scalar.copy)
            if i + 1 < WHOLE_TILES:
                look_up(i + 1)
            else:
                look_up_late(*late[0])
            upper(i)
            for filler in fillers.get(i, []):
                filler()
            minimum(i, 0, first[i], weighed[i])
            if i + 1 < WHOLE_TILES:
                weigh(i + 1)
            minimum(i, 1, third[i], high[i])
            if coming < TILES:
                empty_on_vector(coming)
            for extra in extras.get(i, []):
                extra()

        look_up_late(*late[1])
        both = ring.tile([P, 2, 3, SIDE], F32, name="third", bufs=3)
        trio[late[2]], trio[late[3]] = both[:, 0], both[:, 1]
        for i, b in late[2:]:
            for place, judge in ((2, 0), (0, 1)):
                pick(trio[i, b][:, place], i, halves[b], judge)
        quarters = [slice(0, P), slice(P, SIDE)]
        for side, cols in zip(sides[1:], quarters):
            for i, b in late[2:]:
                pick(trio[i, b][:, 1, cols], i, side, 2)
        weigh_late(*late[0])
        z_codes[1] = keep.tile([P, PICKS], U32, name="weighed", align_bytes=64)
        quantise_z(1, whole)
        second_product(1, sides[0])
        for side in sides[1:]:
            for earlier in range(last):
                second_product(earlier, side)
        upper_late(*late[0])
        minima_late(*late[0], which=slice(0, 1))
        weigh_late(*late[1])
        minima_late(*late[0], which=slice(1, 2))
        upper_late(*late[1])
        minima_late(*late[1], which=slice(0, 1))
        minima_late(*late[1], which=slice(1, 2))
        weigh_late(*late[2])
        median(last, sides[0])
        upper_late(*late[2])
        weigh_late(*late[3])
        quantise_z(last, sides[0])
        second_product(last, sides[0])
        store(sides[0])
        upper_late(*late[3])
        minima_late(*late[2], quarters[0])
        minima_late(*late[3], quarters[0])
        minima_late(*late[2], quarters[1])
        median(last, sides[1])
        minima_late(*late[3], quarters[1])
        quantise_z(last, sides[1])
        second_product(last, sides[1])
        median(last, sides[2])
        quantise_z(last, sides[2])
        second_product(last, sides[2])
        for side in sides[1:]:
            store(side)
